import numpy as np
import ml_dtypes


def mxq(x, axis, fmt="e4m3"):
    dtype, down = {"e4m3": (ml_dtypes.float8_e4m3fn, 7), "e5m2": (ml_dtypes.float8_e5m2, 14)}[fmt]
    v = np.moveaxis(np.asarray(x, np.float32).astype(ml_dtypes.bfloat16).astype(np.float64), axis, -1)
    blocks = v.reshape(v.shape[:-1] + (-1, 32))
    amax = np.abs(blocks).max(-1, keepdims=True)
    byte = np.maximum(np.where(amax > 0, np.frexp(amax)[1] - 1 + 127, 0) - down, 1)
    scale = np.exp2(byte - 127.0)
    codes = (blocks / scale).astype(np.float32).astype(dtype).astype(np.float64)
    return np.moveaxis((codes * scale).reshape(v.shape), -1, axis)


WIDE = False


def mx_kscale(k):
    if not WIDE:
        return np.ones(k)
    levels = np.array([10, -10, 5, -5, 0])
    if k % 512:
        return np.exp2(np.random.permutation(np.resize(levels, k // 32))).repeat(32)
    a = np.empty((k // 512, 16))
    for p in range(k // 512):
        a[p, :8] = np.random.permutation(np.resize(levels, 8))
        for g in range(8):
            far = levels[np.abs(levels - a[p, g]) >= 10]
            a[p, g + 8] = far[np.random.randint(len(far))]
    return np.exp2(a.ravel()).repeat(32)


BF16 = ml_dtypes.bfloat16


def bf(x):
    return np.asarray(x, np.float32).astype(BF16)


def f64(x):
    return np.asarray(x).astype(np.float64)


B, D, F, K = 1024, 512, 1024, 2


def draw0():
    u, t = mx_kscale(D), mx_kscale(F)
    return {
        "x": bf(np.random.standard_normal((B, D)) * u),
        "cs": bf(np.random.standard_normal((K, D, F)) / np.sqrt(D) / u[None, :, None]),
        "ss": bf(np.random.standard_normal((K, D, F)) / np.sqrt(D) / u[None, :, None]),
        "gamma": bf(np.random.uniform(0.5, 1.5, (K, F))),
        "g": bf((1.0 + 0.1 * np.random.standard_normal(F)) * t),
        "dv": bf(np.random.standard_normal((F, D)) / np.sqrt(F) / t[:, None]),
    }


def weno_alpha(s, gamma_k):
    d = 0.5 + s * s
    return gamma_k / (d * d)


def burgers_flux(qh):
    return qh + 0.5 * qh * qh


def core(x, cs, ss, gamma, g, dv):
    cs, ss, gamma, g = f64(cs), f64(ss), f64(gamma), f64(g)
    xq = mxq(f64(x), 1, "e4m3")
    q = [(xq @ mxq(cs[k], 0, "e4m3")) for k in range(K)]
    s = [(xq @ mxq(ss[k], 0, "e4m3")) for k in range(K)]
    al = [weno_alpha(s[k], gamma[k][None, :]) for k in range(K)]
    qh = (al[0] * q[0] + al[1] * q[1]) / (al[0] + al[1])
    phi = burgers_flux(qh)
    pg = phi * g[None, :]
    return mxq(pg, 1, "e4m3") @ mxq(f64(dv), 0, "e4m3")


def e4m3fn_bytes(y):
    return np.clip(np.asarray(y, np.float64), -448.0, 448.0).astype(np.float32).astype(ml_dtypes.float8_e4m3fn).view(np.uint8)


def e4m3fn_values(b):
    return np.asarray(b, np.uint8).view(ml_dtypes.float8_e4m3fn).astype(np.float64)


def setup_inputs():
    d = draw0()
    x0 = np.asarray(d['ss']).astype(np.float64)
    s = (np.max(np.abs(x0), axis=(0, 2), keepdims=True) / 448.0).astype(np.float32)
    out = {}
    for k, v in d.items():
        if k == 'ss':
            out['ss_bytes'] = e4m3fn_bytes(x0 / s.astype(np.float64))
            out['ss_scale'] = s
        else:
            out[k] = v
    return out


def reference(x, cs, ss_bytes, ss_scale, gamma, g, dv):
    return core(x, cs, e4m3fn_values(ss_bytes) * ss_scale.astype(np.float64), gamma, g, dv)

@@ -1,0 +1,404 @@
+from contextlib import ExitStack
+
+import concourse.mybir as mybir
+from concourse.masks import make_identity
+
+B, D, F = 1024, 512, 1024
+FLOPS = 5 * 2 * B * D * F
+
+F32 = mybir.dt.float32
+BF16 = mybir.dt.bfloat16
+U32 = mybir.dt.uint32
+U8 = mybir.dt.uint8
+FP8 = mybir.dt.float8_e4m3fn
+FP8X4 = mybir.dt.float8_e4m3fn_x4
+ALU = mybir.AluOpType
+ACT = mybir.ActivationFunctionType
+
+P = 128
+T = 4
+H = 512
+UNITS = [(h, g, t) for h in range(2) for g in range(2) for t in range(T)]
+BATCHES = (8, 5, 3)
+
+
+def tile_learnedstencilwenostep_kernel(tc, x, cs, ss_bytes, ss_scale, gamma, g, dv, out):
+    nc = tc.nc
+    gain = g
+    with ExitStack() as ctx:
+        keep = ctx.enter_context(tc.tile_pool(name="keep", bufs=1))
+        stage = ctx.enter_context(tc.tile_pool(name="stage", bufs=3))
+        psum_s = ctx.enter_context(tc.psum_pool(name="psum_s", bufs=4))
+        psum_q = ctx.enter_context(tc.psum_pool(name="psum_q", bufs=4))
+
+        ident = keep.tile([P, P], F32, name="ident")
+        warm = keep.tile([P, 1], F32, name="warm")
+        rows = keep.tile([P, H], BF16, name="rows")
+        rows32 = keep.tile([P, T, P], F32, name="rows32")
+        prm = keep.tile([P, 6, T], F32, name="prm")
+        lng = keep.tile([P, 4, T], F32, name="lng")
+        cbias = keep.tile([P, 2, T], F32, name="cbias")
+        ghalf = keep.tile([P, 2, T], F32, name="ghalf")
+        sc = keep.tile([P, T], F32, name="sc")
+        x_raw = [keep.tile([P, T, D], BF16, name=f"x_raw{h}") for h in range(2)]
+        ss_raw = [keep.tile([P, T, F], U8, name=f"ss_raw{k}") for k in range(2)]
+        cs_raw = [keep.tile([P, T, F], BF16, name=f"cs_raw{k}") for k in range(2)]
+        dv_raw = keep.tile([P, 2, T, D], BF16, name="dv_raw")
+        names = ["x0", "x1", "s0g0", "s0g1", "s1g0", "s1g1", "n0t0", "n0t1", "c1g0", "c1g1", "dvg0", "dvg1"]
+        names += [f"pg{h}{gg}" for h in range(2) for gg in range(2)]
+        codes = {n: keep.tile([P, H], U32, name="codes_" + n, align_bytes=64) for n in names}
+        scales = {n: keep.tile([P, H], U8, name="scales_" + n, align_bytes=64) for n in names}
+        dl = [keep.tile([P, H], F32, name=f"dl{u}") for u in range(16)]
+
+        make_identity(nc, ident[:])
+        nc.gpsimd.memset(rows[:], 0.0)
+        nc.vector.memset(warm[:], 1.0)
+
+        nc.sync.dma_start(out=sc[:], in_=ss_scale.rearrange("o (p j) q -> p (o j q)", j=T))
+        nc.sync.dma_start(out=rows[0:4, :], in_=gamma.rearrange("v (g f) -> (v g) f", g=2))
+        nc.sync.dma_start(out=rows[4:6, :], in_=gain.rearrange("(g f) -> g f", g=2))
+        nc.sync.dma_start(out=ss_raw[0][:], in_=ss_bytes[0].rearrange("(p j) f -> p j f", j=T))
+        nc.sync.dma_start(out=x_raw[0][:], in_=x[0:H, :].rearrange("(r i) k -> r i k", i=T))
+        nc.sync.dma_start(out=ss_raw[1][:], in_=ss_bytes[1].rearrange("(p j) f -> p j f", j=T))
+        for k in range(2):
+            nc.sync.dma_start(out=cs_raw[k][:], in_=cs[k].rearrange("(p j) f -> p j f", j=T))
+        nc.sync.dma_start(out=x_raw[1][:], in_=x[H:B, :].rearrange("(r i) k -> r i k", i=T))
+        dv_view = dv.rearrange("(g a t b) n -> g t a b n", g=2, t=T, b=8)
+        for gg in range(2):
+            for t in range(T):
+                nc.sync.dma_start(out=dv_raw[:, gg, t, :], in_=dv_view[gg, t])
+
+        def grouped_tile():
+            return stage.tile([P, 4 * H], BF16, name="grouped", tag="grouped", bufs=6, align_bytes=64)
+
+        grouped = {}
+
+        def quant(n):
+            nc.vector.quantize_mx(out=codes[n][:].bitcast(FP8X4), scales=scales[n][:], in_=grouped[n][:])
+
+        def mm(acc, l, lcols, r, start, stop):
+            nc.tensor.matmul_mx(
+                out=acc,
+                lhsT=codes[l][:, lcols].bitcast(FP8X4), lhsT_scale=scales[l][:, lcols],
+                rhs=codes[r][:].bitcast(FP8X4), rhs_scale=scales[r][:],
+                start=start, stop=stop,
+            )
+
+        xbank = {}
+
+        def x_transpose(h, i2):
+            bank = psum_s.tile([P, 2, 2, P], F32, name="ps", tag="ps")
+            for i in range(2):
+                words = x_raw[h][:, 2 * i2 + i, :].bitcast(F32)
+                for w in range(2):
+                    nc.tensor.transpose(bank[:, i, w, :], words[:, w::2], ident[:])
+            xbank[i2] = bank
+
+        def x_copy(h, i2, engine):
+            n = f"x{h}"
+            if i2 == 0:
+                grouped[n] = grouped_tile()
+            dst = grouped[n][:].bitcast(F32)[:, i2 * H : (i2 + 1) * H]
+            copy = nc.scalar.copy if engine == "s" else nc.vector.tensor_copy
+            copy(out=dst.rearrange("p (i r w) -> p i r w", i=2, w=2), in_=xbank[i2][:].rearrange("p i w r -> p i r w"))
+
+        wide = {}
+
+        def widen(k, gg, engines):
+            wt = stage.tile([P, T, H], BF16, name="wide", tag="wide", bufs=3)
+            wide[k, gg] = wt
+            for j in range(T):
+                engine = engines[j]
+                src = ss_raw[k][:, j, gg * H : (gg + 1) * H].bitcast(FP8)
+                if engine == "s":
+                    nc.scalar.activation(out=wt[:, j, :], in_=src, func=ACT.Copy, scale=sc[:, j : j + 1])
+                else:
+                    nc.vector.tensor_scalar(out=wt[:, j, :], in0=src, scalar1=sc[:, j : j + 1], scalar2=None, op0=ALU.mult)
+
+        def interleave(n, src):
+            gt = grouped_tile()
+            grouped[n] = gt
+            nc.vector.tensor_copy(
+                out=gt[:].rearrange("p (t a b j) -> p t a j b", t=T, b=8, j=T),
+                in_=src.rearrange("p j (a t b) -> p t a j b", t=T, b=8),
+            )
+
+        def ss_inter(k, gg):
+            interleave(f"s{k}g{gg}", wide[k, gg][:])
+
+        def ss_inter_t(t2):
+            if t2 == 0:
+                grouped["s0g0"] = grouped_tile()
+            lo = t2 * 2
+            nc.vector.tensor_copy(
+                out=grouped["s0g0"][:].rearrange("p (t a b j) -> p t a j b", t=T, b=8, j=T)[:, lo : lo + 2],
+                in_=wide[0, 0][:].rearrange("p j (a t b) -> p t a j b", t=T, b=8)[:, lo : lo + 2],
+            )
+
+        def quant_t(t2):
+            lo = t2 * 2 * P
+            nc.vector.quantize_mx(
+                out=codes["s0g0"][:, lo : lo + 2 * P].bitcast(FP8X4), scales=scales["s0g0"][:, lo : lo + 2 * P],
+                in_=grouped["s0g0"][:, 4 * lo : 4 * (lo + 2 * P)],
+            )
+
+        def cs_inter(gg):
+            interleave(f"c1g{gg}", cs_raw[1][:, :, gg * H : (gg + 1) * H])
+
+        def n0_inter(t2):
+            gt = grouped_tile()
+            grouped[f"n0t{t2}"] = gt
+            s5 = cs_raw[0][:].rearrange("p j (a t b) -> p t a j b", t=T, b=8)
+            d5 = gt[:].rearrange("p (t a b j) -> p t a j b", t=2, b=8, j=T)
+            for t in range(2):
+                nc.vector.tensor_scalar(out=d5[:, t], in0=s5[:, 2 * t2 + t], scalar1=-1.0, scalar2=None, op0=ALU.mult)
+
+        def dv_inter(gg):
+            n = f"dvg{gg}"
+            gt = grouped_tile()
+            grouped[n] = gt
+            return gt
+
+        def dv_piece(gg, q):
+            if q == 0:
+                dv_inter(gg)
+            w = D // 4
+            nc.gpsimd.tensor_scalar(
+                out=grouped[f"dvg{gg}"][:, 4 * q * w : 4 * (q + 1) * w].rearrange("p (c i t) -> p c t i", i=8, t=T),
+                in0=dv_raw[:, gg, :, q * w : (q + 1) * w].rearrange("p t (c i) -> p c t i", i=8),
+                scalar1=1.0, scalar2=0.0, op0=ALU.mult, op1=ALU.add,
+            )
+
+        sbank = {}
+        ul = {}
+
+        def mm_s(u, k):
+            h, gg, t = UNITS[u]
+            acc = psum_s.tile([P, H], F32, name="ps", tag="ps")
+            sbank[u, k] = acc
+            mm(acc[:], f"s{k}g{gg}", slice(t * P, (t + 1) * P), f"x{h}", True, True)
+
+        def sq(u, k):
+            if k == 0:
+                ul[u] = stage.tile([P, 2, H], F32, name="ul", tag="ul", bufs=5)
+            nc.scalar.activation(out=ul[u][:, k, :], in_=sbank[u, k][:], func=ACT.Square)
+
+        def ln(u):
+            nc.scalar.activation(out=ul[u][:], in_=ul[u][:], func=ACT.Ln, bias=0.5, scale=1.0)
+
+        def delta(u):
+            nc.vector.tensor_tensor(out=dl[u][:], in0=ul[u][:, 0, :], in1=ul[u][:, 1, :], op=ALU.subtract)
+
+        def sig(u):
+            h, gg, t = UNITS[u]
+            nc.scalar.activation(out=dl[u][:], in_=dl[u][:], func=ACT.Sigmoid, bias=cbias[:, gg, t : t + 1], scale=2.0)
+
+        nbank, dbank, mt, qh, zz, pg = {}, {}, {}, {}, {}, {}
+
+        def mm_q(u):
+            h, gg, t = UNITS[u]
+            cols = slice(t * P, (t + 1) * P)
+            ncols = slice((t % 2 * 2 + gg) * P, (t % 2 * 2 + gg + 1) * P)
+            dbank[u] = psum_q.tile([P, H], F32, name="pq", tag="pq")
+            mm(dbank[u][:], f"c1g{gg}", cols, f"x{h}", True, False)
+            mm(dbank[u][:], f"n0t{t // 2}", ncols, f"x{h}", False, True)
+            nbank[u] = psum_q.tile([P, H], F32, name="pq", tag="pq")
+            mm(nbank[u][:], f"n0t{t // 2}", ncols, f"x{h}", True, True)
+
+        def wd(u):
+            mt[u] = stage.tile([P, H], F32, name="mt", tag="mt", bufs=3)
+            nc.vector.tensor_tensor(out=mt[u][:], in0=dbank[u][:], in1=dl[u][:], op=ALU.mult)
+
+        def sub(u):
+            h, gg, t = UNITS[u]
+            if t == 0:
+                qh[h, gg] = stage.tile([P, T, H], F32, name="qh", tag="qh", bufs=2)
+                zz[h, gg] = stage.tile([P, T, H], F32, name="zz", tag="zz", bufs=2)
+            nc.vector.tensor_tensor(out=qh[h, gg][:, t, :], in0=mt[u][:], in1=nbank[u][:], op=ALU.subtract)
+
+        def zf(u):
+            h, gg, t = UNITS[u]
+            if u >= 13:
+                nc.scalar.activation(
+                    out=zz[h, gg][:, t, :], in_=qh[h, gg][:, t, :], func=ACT.Identity,
+                    scale=ghalf[:, gg, t : t + 1], bias=prm[:, 4 + gg, t : t + 1],
+                )
+                return
+            nc.gpsimd.tensor_scalar(
+                out=zz[h, gg][:, t, :], in0=qh[h, gg][:, t, :],
+                scalar1=ghalf[:, gg, t : t + 1], scalar2=prm[:, 4 + gg, t : t + 1], op0=ALU.mult, op1=ALU.add,
+            )
+
+        def mul(h, gg, part, parts):
+            n = f"pg{h}{gg}"
+            if part == 0:
+                grouped[n] = grouped_tile()
+            w = H // parts
+            lo = part * w
+            nc.vector.tensor_tensor(
+                out=grouped[n][:, 4 * lo : 4 * (lo + w)].rearrange("p (c i t) -> p c t i", i=4, t=T),
+                in0=zz[h, gg][:, :, lo : lo + w].rearrange("p t (c i) -> p c t i", i=4),
+                in1=qh[h, gg][:, :, lo : lo + w].rearrange("p t (c i) -> p c t i", i=4),
+                op=ALU.mult,
+            )
+
+        def pquant(h, gg, part, parts):
+            n = f"pg{h}{gg}"
+            w = H // parts
+            lo = part * w
+            nc.vector.quantize_mx(
+                out=codes[n][:, lo : lo + w].bitcast(FP8X4), scales=scales[n][:, lo : lo + w],
+                in_=grouped[n][:, 4 * lo : 4 * (lo + w)],
+            )
+
+        out_view = out.rearrange("(h r i) d -> h i r d", h=2, i=T)
+        obank = {}
+
+        def mm_o(h, i, gg):
+            if gg == 0:
+                obank[h, i] = psum_q.tile([P, D], F32, name="pq", tag="pq")
+            mm(obank[h, i][:], f"pg{h}{gg}", slice(i * P, (i + 1) * P), f"dvg{gg}", gg == 0, gg == 1)
+
+        def o_copy(h, i, engine):
+            ot = stage.tile([P, D], F32, name="ot", tag="ot", bufs=4)
+            if engine == "s":
+                nc.scalar.copy(out=ot[:], in_=obank[h, i][:])
+            else:
+                nc.vector.tensor_copy(out=ot[:], in_=obank[h, i][:])
+            nc.sync.dma_start(out=out_view[h, i], in_=ot[:])
+
+        def params_a():
+            nc.gpsimd.tensor_scalar(
+                out=rows32[:].rearrange("p t (a b) -> p t a b", b=8), in0=rows[:].rearrange("p (a t b) -> p t a b", t=T, b=8),
+                scalar1=1.0, scalar2=0.0, op0=ALU.mult, op1=ALU.add,
+            )
+            bank = psum_s.tile([P, T, P], F32, name="ps", tag="ps")
+            for t in range(T):
+                nc.tensor.transpose(bank[:, t, :], rows32[:, t, :], ident[:])
+            nc.scalar.copy(out=prm[:], in_=bank[:, :, 0:6].rearrange("p t r -> p r t"))
+
+        def params_b():
+            nc.vector.tensor_scalar(out=lng[:], in0=prm[:, 0:4, :], scalar1=2.0**-64, scalar2=None, op0=ALU.max)
+            nc.vector.tensor_scalar(out=ghalf[:], in0=prm[:, 4:6, :], scalar1=0.5, scalar2=None, op0=ALU.mult)
+
+        def params_c():
+            nc.scalar.activation(out=lng[:], in_=lng[:], func=ACT.Ln)
+
+        def params_d():
+            nc.vector.tensor_tensor(out=cbias[:], in0=lng[:, 2:4, :], in1=lng[:, 0:2, :], op=ALU.subtract)
+
+        def q_stream(us, parts=1):
+            steps = []
+            n = len(us)
+            for j in range(n + 2):
+                st = []
+                if j < n:
+                    st.append(lambda u=us[j]: (mm_q(u), wd(u)))
+                if 1 <= j <= n:
+                    st.append(lambda u=us[j - 1]: (sub(u), zf(u)))
+                if j >= 2 and UNITS[us[j - 2]][2] == 3:
+                    h, gg, t = UNITS[us[j - 2]]
+                    for q in range(parts):
+                        st.append(lambda h=h, gg=gg, q=q: mul(h, gg, q, parts))
+                    for q in range(parts):
+                        st.append(lambda h=h, gg=gg, q=q: pquant(h, gg, q, parts))
+                steps.append(st)
+            return steps
+
+        def s_stream(us):
+            steps = []
+            n = len(us)
+            for j in range(n + 1):
+                st = []
+                if j < n:
+                    st.append(lambda u=us[j]: (mm_s(u, 0), sq(u, 0), mm_s(u, 1), sq(u, 1)))
+                if j >= 1:
+                    st.append(lambda u=us[j - 1]: ln(u))
+                steps.append(st)
+            return steps
+
+        def d_stream(us, lag):
+            return [[] for _ in range(lag)] + [[lambda u=u: delta(u)] for u in us]
+
+        def weave(*streams):
+            for j in range(max(len(s) for s in streams)):
+                for s in streams:
+                    for f in (s[j] if j < len(s) else ()):
+                        f()
+
+        def out_tile(h, i, engine):
+            mm_o(h, i, 0)
+            mm_o(h, i, 1)
+            o_copy(h, i, engine)
+
+        b1 = list(range(BATCHES[0]))
+        b2 = list(range(BATCHES[0], BATCHES[0] + BATCHES[1]))
+        b3 = list(range(BATCHES[0] + BATCHES[1], 16))
+
+        with tc.manual_schedule():
+            nc.scalar.activation(out=warm[:], in_=warm[:], func=ACT.Ln)
+            widen(0, 0, "vvss")
+            ss_inter_t(0)
+            for i2 in range(2):
+                x_transpose(0, i2)
+                x_copy(0, i2, "s")
+            quant_t(0)
+            quant("x0")
+            widen(1, 0, "ssvv")
+            params_a()
+            for u in range(2):
+                mm_s(u, 0)
+                sq(u, 0)
+            ss_inter_t(1)
+            quant_t(1)
+            for u in range(2, 4):
+                mm_s(u, 0)
+                sq(u, 0)
+            ss_inter(1, 0)
+            quant("s1g0")
+            for u in range(4):
+                mm_s(u, 1)
+                sq(u, 1)
+            for u in range(4):
+                ln(u)
+            widen(0, 1, "vvvv")
+            ss_inter(0, 1)
+            params_b()
+            quant("s0g1")
+            widen(1, 1, "vvvv")
+            ss_inter(1, 1)
+            quant("s1g1")
+            cs_inter(0)
+            delta(0)
+            quant("c1g0")
+            n0_inter(0)
+            delta(1)
+            quant("n0t0")
+            params_c()
+            weave(s_stream(b1[4:]))
+            n0_inter(1)
+            params_d()
+            delta(2)
+            quant("n0t1")
+            for u in b1[3:]:
+                delta(u)
+            for u in b1:
+                sig(u)
+            for i2 in range(2):
+                x_transpose(1, i2)
+                x_copy(1, i2, "v")
+            cs_inter(1)
+            quant("x1")
+            prep = [[lambda: quant("c1g1")]]
+            dvp = [[]] + [[lambda q=q: dv_piece(q // 4, q % 4)] for q in range(8)]
+            weave(s_stream(b2), q_stream(b1), dvp, prep, d_stream(b2, 2))
+            for u in b2:
+                sig(u)
+            quant("dvg0")
+            quant("dvg1")
+            weave(s_stream(b3), q_stream(b2), d_stream(b3, 4))
+            for u in b3:
+                sig(u)
+            weave(q_stream(b3, 2), [[lambda i=i: out_tile(0, i, "s")] for i in range(T)])
+            for i in range(T):
+                out_tile(1, i, "sv"[i % 2])

@@ -20,6 +20,8 @@ T = 4
 H = 512
 UNITS = [(h, g, t) for h in range(2) for g in range(2) for t in range(T)]
 BATCHES = (8, 5, 3)
+S_GAIN = 13
+S_BANKS = 3
 
 
 def tile_learnedstencilwenostep_kernel(tc, x, cs, ss_bytes, ss_scale, gamma, g, dv, out):
@@ -28,8 +30,8 @@ def tile_learnedstencilwenostep_kernel(tc, x, cs, ss_bytes, ss_scale, gamma, g, 
     with ExitStack() as ctx:
         keep = ctx.enter_context(tc.tile_pool(name="keep", bufs=1))
         stage = ctx.enter_context(tc.tile_pool(name="stage", bufs=3))
-        psum_s = ctx.enter_context(tc.psum_pool(name="psum_s", bufs=4))
-        psum_q = ctx.enter_context(tc.psum_pool(name="psum_q", bufs=4))
+        psum_s = ctx.enter_context(tc.psum_pool(name="psum_s", bufs=S_BANKS))
+        psum_q = ctx.enter_context(tc.psum_pool(name="psum_q", bufs=8 - S_BANKS))
 
         ident = keep.tile([P, P], F32, name="ident")
         warm = keep.tile([P, 1], F32, name="warm")
@@ -55,11 +57,13 @@ def tile_learnedstencilwenostep_kernel(tc, x, cs, ss_bytes, ss_scale, gamma, g, 
         nc.vector.memset(warm[:], 1.0)
 
         nc.sync.dma_start(out=sc[:], in_=ss_scale.rearrange("o (p j) q -> p (o j q)", j=T))
+        x_half = x[0:H, :].rearrange("(r i) k -> r i k", i=T)
+        nc.sync.dma_start(out=x_raw[0][:, 0:2, :], in_=x_half[:, 0:2, :])
+        nc.sync.dma_start(out=ss_raw[0][:], in_=ss_bytes[0].rearrange("(p j) f -> p j f", j=T))
+        nc.sync.dma_start(out=x_raw[0][:, 2:4, :], in_=x_half[:, 2:4, :])
+        nc.sync.dma_start(out=ss_raw[1][:], in_=ss_bytes[1].rearrange("(p j) f -> p j f", j=T))
         nc.sync.dma_start(out=rows[0:4, :], in_=gamma.rearrange("v (g f) -> (v g) f", g=2))
         nc.sync.dma_start(out=rows[4:6, :], in_=gain.rearrange("(g f) -> g f", g=2))
-        nc.sync.dma_start(out=ss_raw[0][:], in_=ss_bytes[0].rearrange("(p j) f -> p j f", j=T))
-        nc.sync.dma_start(out=x_raw[0][:], in_=x[0:H, :].rearrange("(r i) k -> r i k", i=T))
-        nc.sync.dma_start(out=ss_raw[1][:], in_=ss_bytes[1].rearrange("(p j) f -> p j f", j=T))
         for k in range(2):
             nc.sync.dma_start(out=cs_raw[k][:], in_=cs[k].rearrange("(p j) f -> p j f", j=T))
         nc.sync.dma_start(out=x_raw[1][:], in_=x[H:B, :].rearrange("(r i) k -> r i k", i=T))
@@ -104,11 +108,11 @@ def tile_learnedstencilwenostep_kernel(tc, x, cs, ss_bytes, ss_scale, gamma, g, 
 
         wide = {}
 
-        def widen(k, gg, engines):
-            wt = stage.tile([P, T, H], BF16, name="wide", tag="wide", bufs=3)
-            wide[k, gg] = wt
-            for j in range(T):
-                engine = engines[j]
+        def widen(k, gg, engine, js=range(T)):
+            if (k, gg) not in wide:
+                wide[k, gg] = stage.tile([P, T, H], BF16, name="wide", tag="wide", bufs=3)
+            wt = wide[k, gg]
+            for j in js:
                 src = ss_raw[k][:, j, gg * H : (gg + 1) * H].bitcast(FP8)
                 if engine == "s":
                     nc.scalar.activation(out=wt[:, j, :], in_=src, func=ACT.Copy, scale=sc[:, j : j + 1])
@@ -173,6 +177,8 @@ def tile_learnedstencilwenostep_kernel(tc, x, cs, ss_bytes, ss_scale, gamma, g, 
         ul = {}
 
         def mm_s(u, k):
+            if (u, k) in sbank:
+                return
             h, gg, t = UNITS[u]
             acc = psum_s.tile([P, H], F32, name="ps", tag="ps")
             sbank[u, k] = acc
@@ -218,13 +224,13 @@ def tile_learnedstencilwenostep_kernel(tc, x, cs, ss_bytes, ss_scale, gamma, g, 
 
         def zf(u):
             h, gg, t = UNITS[u]
-            if u >= 13:
+            if u >= S_GAIN and u < 15:
                 nc.scalar.activation(
                     out=zz[h, gg][:, t, :], in_=qh[h, gg][:, t, :], func=ACT.Identity,
                     scale=ghalf[:, gg, t : t + 1], bias=prm[:, 4 + gg, t : t + 1],
                 )
                 return
-            nc.gpsimd.tensor_scalar(
+            (nc.vector if u == 15 else nc.gpsimd).tensor_scalar(
                 out=zz[h, gg][:, t, :], in0=qh[h, gg][:, t, :],
                 scalar1=ghalf[:, gg, t : t + 1], scalar2=prm[:, 4 + gg, t : t + 1], op0=ALU.mult, op1=ALU.add,
             )
@@ -287,44 +293,6 @@ def tile_learnedstencilwenostep_kernel(tc, x, cs, ss_bytes, ss_scale, gamma, g, 
         def params_d():
             nc.vector.tensor_tensor(out=cbias[:], in0=lng[:, 2:4, :], in1=lng[:, 0:2, :], op=ALU.subtract)
 
-        def q_stream(us, parts=1):
-            steps = []
-            n = len(us)
-            for j in range(n + 2):
-                st = []
-                if j < n:
-                    st.append(lambda u=us[j]: (mm_q(u), wd(u)))
-                if 1 <= j <= n:
-                    st.append(lambda u=us[j - 1]: (sub(u), zf(u)))
-                if j >= 2 and UNITS[us[j - 2]][2] == 3:
-                    h, gg, t = UNITS[us[j - 2]]
-                    for q in range(parts):
-                        st.append(lambda h=h, gg=gg, q=q: mul(h, gg, q, parts))
-                    for q in range(parts):
-                        st.append(lambda h=h, gg=gg, q=q: pquant(h, gg, q, parts))
-                steps.append(st)
-            return steps
-
-        def s_stream(us):
-            steps = []
-            n = len(us)
-            for j in range(n + 1):
-                st = []
-                if j < n:
-                    st.append(lambda u=us[j]: (mm_s(u, 0), sq(u, 0), mm_s(u, 1), sq(u, 1)))
-                if j >= 1:
-                    st.append(lambda u=us[j - 1]: ln(u))
-                steps.append(st)
-            return steps
-
-        def d_stream(us, lag):
-            return [[] for _ in range(lag)] + [[lambda u=u: delta(u)] for u in us]
-
-        def weave(*streams):
-            for j in range(max(len(s) for s in streams)):
-                for s in streams:
-                    for f in (s[j] if j < len(s) else ()):
-                        f()
 
         def out_tile(h, i, engine):
             mm_o(h, i, 0)
@@ -335,70 +303,142 @@ def tile_learnedstencilwenostep_kernel(tc, x, cs, ss_bytes, ss_scale, gamma, g, 
         b2 = list(range(BATCHES[0], BATCHES[0] + BATCHES[1]))
         b3 = list(range(BATCHES[0] + BATCHES[1], 16))
 
+        def s_unit(u):
+            mm_s(u, 0)
+            mm_s(u, 1)
+            sq(u, 0)
+            sq(u, 1)
+
         with tc.manual_schedule():
             nc.scalar.activation(out=warm[:], in_=warm[:], func=ACT.Ln)
-            widen(0, 0, "vvss")
+            x_transpose(0, 0)
+            x_copy(0, 0, "s")
+            widen(0, 0, "v", (0, 1))
+            widen(0, 0, "s", (2, 3))
+            x_transpose(0, 1)
+            x_copy(0, 1, "s")
+            widen(1, 0, "s", (0, 1))
             ss_inter_t(0)
-            for i2 in range(2):
-                x_transpose(0, i2)
-                x_copy(0, i2, "s")
-            quant_t(0)
             quant("x0")
-            widen(1, 0, "ssvv")
-            params_a()
+            quant_t(0)
             for u in range(2):
                 mm_s(u, 0)
                 sq(u, 0)
             ss_inter_t(1)
+            widen(1, 0, "v", (2, 3))
             quant_t(1)
             for u in range(2, 4):
                 mm_s(u, 0)
                 sq(u, 0)
             ss_inter(1, 0)
+            widen(0, 1, "v", (0, 1))
             quant("s1g0")
             for u in range(4):
                 mm_s(u, 1)
                 sq(u, 1)
-            for u in range(4):
-                ln(u)
-            widen(0, 1, "vvvv")
+            ln(0)
+            ln(1)
+            ln(2)
+            widen(0, 1, "v", (2, 3))
             ss_inter(0, 1)
-            params_b()
+            widen(1, 1, "v")
             quant("s0g1")
-            widen(1, 1, "vvvv")
             ss_inter(1, 1)
-            quant("s1g1")
-            cs_inter(0)
+            params_a()
             delta(0)
-            quant("c1g0")
-            n0_inter(0)
+            quant("s1g1")
+            mm_s(4, 0)
+            sq(4, 0)
+            ln(3)
             delta(1)
-            quant("n0t0")
-            params_c()
-            weave(s_stream(b1[4:]))
-            n0_inter(1)
-            params_d()
+            n0_inter(0)
             delta(2)
-            quant("n0t1")
-            for u in b1[3:]:
-                delta(u)
-            for u in b1:
-                sig(u)
+            quant("n0t0")
+            mm_s(4, 1)
+            sq(4, 1)
+            s_unit(5)
+            ln(4)
+            s_unit(6)
+            ln(5)
+            params_b()
+            params_c()
+            cs_inter(0)
+            delta(3)
+            quant("c1g0")
             for i2 in range(2):
                 x_transpose(1, i2)
                 x_copy(1, i2, "v")
-            cs_inter(1)
+            n0_inter(1)
             quant("x1")
-            prep = [[lambda: quant("c1g1")]]
-            dvp = [[]] + [[lambda q=q: dv_piece(q // 4, q % 4)] for q in range(8)]
-            weave(s_stream(b2), q_stream(b1), dvp, prep, d_stream(b2, 2))
-            for u in b2:
+            params_d()
+            delta(4)
+            quant("n0t1")
+            s_unit(7)
+            ln(6)
+            ln(7)
+            delta(5)
+            cs_inter(1)
+            delta(6)
+            delta(7)
+            quant("c1g1")
+            for u in b1:
                 sig(u)
+            LEAD = 3
+            def blend(us, s_us, lead, d_at, dv=False, pend=[]):
+                n = len(us)
+                d_at = dict(d_at)
+                sdone = 0
+                for j in range(n + 3):
+                    if j < n:
+                        mm_q(us[j])
+                    if lead <= j < lead + len(s_us):
+                        s_unit(s_us[j - lead])
+                    if lead + 1 <= j < lead + 1 + len(s_us):
+                        ln(s_us[j - lead - 1])
+                    for u in d_at.get(j, ()):
+                        delta(u)
+                    if j < n:
+                        wd(us[j])
+                    if j >= 3 and UNITS[us[j - 3]][2] == 3:
+                        h, gg, t = UNITS[us[j - 3]]
+                        mul(h, gg, 0, 1)
+                    if 1 <= j <= n:
+                        sub(us[j - 1])
+                        zf(us[j - 1])
+                        if dv and 1 <= j <= 8:
+                            dv_piece((j - 1) // 4, (j - 1) % 4)
+                    if j >= 3 and UNITS[us[j - 3]][2] == 3:
+                        pquant(h, gg, 0, 1)
+                for j in range(len(s_us)):
+                    pass
+            mm_s(8, 0)
+            mm_s(8, 1)
+            mm_s(9, 0)
+            blend(b1, b2, 3, {7: [8], 8: [9], 9: [10], 10: [11, 12]}, True)
             quant("dvg0")
             quant("dvg1")
-            weave(s_stream(b3), q_stream(b2), d_stream(b3, 4))
+            for u in b2:
+                sig(u)
+            mm_s(13, 0)
+            mm_s(13, 1)
+            mm_s(14, 0)
+            blend(b2, b3, 0, {5: [13], 6: [14], 7: [15]})
             for u in b3:
                 sig(u)
-            weave(q_stream(b3, 2), [[lambda i=i: out_tile(0, i, "s")] for i in range(T)])
+            for j, u in enumerate(b3 + [None]):
+                if u is not None:
+                    mm_q(u)
+                out_tile(0, j, "s")
+                if u is not None:
+                    wd(u)
+                if j:
+                    sub(b3[j - 1])
+                    zf(b3[j - 1])
             for i in range(T):
-                out_tile(1, i, "sv"[i % 2])
+                mm_o(1, i, 0)
+            for part in range(2):
+                mul(1, 1, part, 2)
+                pquant(1, 1, part, 2)
+            for i in range(T):
+                mm_o(1, i, 1)
+                o_copy(1, i, "sssv"[i])

@@ -19,8 +19,6 @@ P = 128
 T = 4
 H = 512
 UNITS = [(h, g, t) for h in range(2) for g in range(2) for t in range(T)]
-BATCHES = (8, 5, 3)
-S_GAIN = 13
 S_BANKS = 3
 
 
@@ -52,7 +50,9 @@ def tile_learnedstencilwenostep_kernel(tc, x, cs, ss_bytes, ss_scale, gamma, g, 
         scales = {n: keep.tile([P, H], U8, name="scales_" + n, align_bytes=64) for n in names}
         dl = [keep.tile([P, H], F32, name=f"dl{u}") for u in range(16)]
 
+        nident = keep.tile([P, P], F32, name="nident")
         make_identity(nc, ident[:])
+        nc.gpsimd.tensor_scalar(out=nident[:], in0=ident[:], scalar1=-1.0, scalar2=0.0, op0=ALU.mult, op1=ALU.add)
         nc.gpsimd.memset(rows[:], 0.0)
         nc.vector.memset(warm[:], 1.0)
 
@@ -80,11 +80,11 @@ def tile_learnedstencilwenostep_kernel(tc, x, cs, ss_bytes, ss_scale, gamma, g, 
         def quant(n):
             nc.vector.quantize_mx(out=codes[n][:].bitcast(FP8X4), scales=scales[n][:], in_=grouped[n][:])
 
-        def mm(acc, l, lcols, r, start, stop):
+        def mm(acc, l, lcols, r, start, stop, tok=slice(0, H)):
             nc.tensor.matmul_mx(
                 out=acc,
                 lhsT=codes[l][:, lcols].bitcast(FP8X4), lhsT_scale=scales[l][:, lcols],
-                rhs=codes[r][:].bitcast(FP8X4), rhs_scale=scales[r][:],
+                rhs=codes[r][:, tok].bitcast(FP8X4), rhs_scale=scales[r][:, tok],
                 start=start, stop=stop,
             )
 
@@ -96,15 +96,15 @@ def tile_learnedstencilwenostep_kernel(tc, x, cs, ss_bytes, ss_scale, gamma, g, 
                 words = x_raw[h][:, 2 * i2 + i, :].bitcast(F32)
                 for w in range(2):
                     nc.tensor.transpose(bank[:, i, w, :], words[:, w::2], ident[:])
-            xbank[i2] = bank
+            xbank[h, i2] = bank
 
         def x_copy(h, i2, engine):
             n = f"x{h}"
-            if i2 == 0:
+            if n not in grouped:
                 grouped[n] = grouped_tile()
             dst = grouped[n][:].bitcast(F32)[:, i2 * H : (i2 + 1) * H]
             copy = nc.scalar.copy if engine == "s" else nc.vector.tensor_copy
-            copy(out=dst.rearrange("p (i r w) -> p i r w", i=2, w=2), in_=xbank[i2][:].rearrange("p i w r -> p i r w"))
+            copy(out=dst.rearrange("p (i r w) -> p i r w", i=2, w=2), in_=xbank[h, i2][:].rearrange("p i w r -> p i r w"))
 
         wide = {}
 
@@ -131,7 +131,7 @@ def tile_learnedstencilwenostep_kernel(tc, x, cs, ss_bytes, ss_scale, gamma, g, 
             interleave(f"s{k}g{gg}", wide[k, gg][:])
 
         def ss_inter_t(t2):
-            if t2 == 0:
+            if "s0g0" not in grouped:
                 grouped["s0g0"] = grouped_tile()
             lo = t2 * 2
             nc.vector.tensor_copy(
@@ -164,7 +164,7 @@ def tile_learnedstencilwenostep_kernel(tc, x, cs, ss_bytes, ss_scale, gamma, g, 
             return gt
 
         def dv_piece(gg, q):
-            if q == 0:
+            if f"dvg{gg}" not in grouped:
                 dv_inter(gg)
             w = D // 4
             nc.gpsimd.tensor_scalar(
@@ -174,11 +174,10 @@ def tile_learnedstencilwenostep_kernel(tc, x, cs, ss_bytes, ss_scale, gamma, g, 
             )
 
         sbank = {}
+        dbk = {}
         ul = {}
 
         def mm_s(u, k):
-            if (u, k) in sbank:
-                return
             h, gg, t = UNITS[u]
             acc = psum_s.tile([P, H], F32, name="ps", tag="ps")
             sbank[u, k] = acc
@@ -195,21 +194,34 @@ def tile_learnedstencilwenostep_kernel(tc, x, cs, ss_bytes, ss_scale, gamma, g, 
         def delta(u):
             nc.vector.tensor_tensor(out=dl[u][:], in0=ul[u][:, 0, :], in1=ul[u][:, 1, :], op=ALU.subtract)
 
+        def pdelta(u):
+            bank = psum_s.tile([P, H], F32, name="ps", tag="ps")
+            nc.tensor.matmul(bank[:], lhsT=ident[:], rhs=ul[u][:, 0, :], start=True, stop=False)
+            nc.tensor.matmul(bank[:], lhsT=nident[:], rhs=ul[u][:, 1, :], start=False, stop=True)
+            dbk[u] = bank
+
         def sig(u):
             h, gg, t = UNITS[u]
-            nc.scalar.activation(out=dl[u][:], in_=dl[u][:], func=ACT.Sigmoid, bias=cbias[:, gg, t : t + 1], scale=2.0)
+            nc.scalar.activation(out=dl[u][:], in_=dbk[u][:] if u in dbk else dl[u][:], func=ACT.Sigmoid, bias=cbias[:, gg, t : t + 1], scale=2.0)
 
-        nbank, dbank, mt, qh, zz, pg = {}, {}, {}, {}, {}, {}
+        nbank, dbank, mt, qh, zz = {}, {}, {}, {}, {}
 
-        def mm_q(u):
+        def q_operands(u):
             h, gg, t = UNITS[u]
             cols = slice(t * P, (t + 1) * P)
-            ncols = slice((t % 2 * 2 + gg) * P, (t % 2 * 2 + gg + 1) * P)
+            n0 = t % 2 * 2 + gg
+            return f"c1g{gg}", cols, f"n0t{t // 2}", slice(n0 * P, (n0 + 1) * P), f"x{h}"
+
+        def mm_d(u):
+            c1, cols, n0, ncols, xx = q_operands(u)
             dbank[u] = psum_q.tile([P, H], F32, name="pq", tag="pq")
-            mm(dbank[u][:], f"c1g{gg}", cols, f"x{h}", True, False)
-            mm(dbank[u][:], f"n0t{t // 2}", ncols, f"x{h}", False, True)
+            mm(dbank[u][:], c1, cols, xx, True, False)
+            mm(dbank[u][:], n0, ncols, xx, False, True)
+
+        def mm_n(u):
+            c1, cols, n0, ncols, xx = q_operands(u)
             nbank[u] = psum_q.tile([P, H], F32, name="pq", tag="pq")
-            mm(nbank[u][:], f"n0t{t // 2}", ncols, f"x{h}", True, True)
+            mm(nbank[u][:], n0, ncols, xx, True, True)
 
         def wd(u):
             mt[u] = stage.tile([P, H], F32, name="mt", tag="mt", bufs=3)
@@ -217,27 +229,24 @@ def tile_learnedstencilwenostep_kernel(tc, x, cs, ss_bytes, ss_scale, gamma, g, 
 
         def sub(u):
             h, gg, t = UNITS[u]
-            if t == 0:
+            if (h, gg) not in qh:
                 qh[h, gg] = stage.tile([P, T, H], F32, name="qh", tag="qh", bufs=2)
                 zz[h, gg] = stage.tile([P, T, H], F32, name="zz", tag="zz", bufs=2)
             nc.vector.tensor_tensor(out=qh[h, gg][:, t, :], in0=mt[u][:], in1=nbank[u][:], op=ALU.subtract)
 
-        def zf(u):
+        def zf(u, engine):
             h, gg, t = UNITS[u]
-            if u >= S_GAIN and u < 15:
-                nc.scalar.activation(
-                    out=zz[h, gg][:, t, :], in_=qh[h, gg][:, t, :], func=ACT.Identity,
-                    scale=ghalf[:, gg, t : t + 1], bias=prm[:, 4 + gg, t : t + 1],
-                )
-                return
-            (nc.vector if u == 15 else nc.gpsimd).tensor_scalar(
-                out=zz[h, gg][:, t, :], in0=qh[h, gg][:, t, :],
-                scalar1=ghalf[:, gg, t : t + 1], scalar2=prm[:, 4 + gg, t : t + 1], op0=ALU.mult, op1=ALU.add,
-            )
+            half, full = ghalf[:, gg, t : t + 1], prm[:, 4 + gg, t : t + 1]
+            dst, src = zz[h, gg][:, t, :], qh[h, gg][:, t, :]
+            if engine == "s":
+                nc.scalar.activation(out=dst, in_=src, func=ACT.Identity, scale=half, bias=full)
+            else:
+                e = nc.vector if engine == "v" else nc.gpsimd
+                e.tensor_scalar(out=dst, in0=src, scalar1=half, scalar2=full, op0=ALU.mult, op1=ALU.add)
 
         def mul(h, gg, part, parts):
             n = f"pg{h}{gg}"
-            if part == 0:
+            if n not in grouped:
                 grouped[n] = grouped_tile()
             w = H // parts
             lo = part * w
@@ -262,7 +271,7 @@ def tile_learnedstencilwenostep_kernel(tc, x, cs, ss_bytes, ss_scale, gamma, g, 
 
         def mm_o(h, i, gg):
             if gg == 0:
-                obank[h, i] = psum_q.tile([P, D], F32, name="pq", tag="pq")
+                obank[h, i] = psum_s.tile([P, D], F32, name="ps", tag="ps")
             mm(obank[h, i][:], f"pg{h}{gg}", slice(i * P, (i + 1) * P), f"dvg{gg}", gg == 0, gg == 1)
 
         def o_copy(h, i, engine):
@@ -273,15 +282,22 @@ def tile_learnedstencilwenostep_kernel(tc, x, cs, ss_bytes, ss_scale, gamma, g, 
                 nc.vector.tensor_copy(out=ot[:], in_=obank[h, i][:])
             nc.sync.dma_start(out=out_view[h, i], in_=ot[:])
 
-        def params_a():
+        def pa_rows():
             nc.gpsimd.tensor_scalar(
                 out=rows32[:].rearrange("p t (a b) -> p t a b", b=8), in0=rows[:].rearrange("p (a t b) -> p t a b", t=T, b=8),
                 scalar1=1.0, scalar2=0.0, op0=ALU.mult, op1=ALU.add,
             )
+
+        pbank = {}
+
+        def pa_turn():
             bank = psum_s.tile([P, T, P], F32, name="ps", tag="ps")
             for t in range(T):
                 nc.tensor.transpose(bank[:, t, :], rows32[:, t, :], ident[:])
-            nc.scalar.copy(out=prm[:], in_=bank[:, :, 0:6].rearrange("p t r -> p r t"))
+            pbank[0] = bank
+
+        def pa_out():
+            nc.scalar.copy(out=prm[:], in_=pbank[0][:, :, 0:6].rearrange("p t r -> p r t"))
 
         def params_b():
             nc.vector.tensor_scalar(out=lng[:], in0=prm[:, 0:4, :], scalar1=2.0**-64, scalar2=None, op0=ALU.max)
@@ -299,146 +315,295 @@ def tile_learnedstencilwenostep_kernel(tc, x, cs, ss_bytes, ss_scale, gamma, g, 
             mm_o(h, i, 1)
             o_copy(h, i, engine)
 
-        b1 = list(range(BATCHES[0]))
-        b2 = list(range(BATCHES[0], BATCHES[0] + BATCHES[1]))
-        b3 = list(range(BATCHES[0] + BATCHES[1], 16))
-
-        def s_unit(u):
-            mm_s(u, 0)
-            mm_s(u, 1)
-            sq(u, 0)
-            sq(u, 1)
-
         with tc.manual_schedule():
             nc.scalar.activation(out=warm[:], in_=warm[:], func=ACT.Ln)
             x_transpose(0, 0)
-            x_copy(0, 0, "s")
-            widen(0, 0, "v", (0, 1))
-            widen(0, 0, "s", (2, 3))
+            x_copy(0, 0, "v")
+            widen(0, 0, "v", (1,))
+            widen(0, 0, "s", (3,))
+            widen(0, 0, "v", (2,))
             x_transpose(0, 1)
-            x_copy(0, 1, "s")
-            widen(1, 0, "s", (0, 1))
-            ss_inter_t(0)
-            quant("x0")
-            quant_t(0)
-            for u in range(2):
-                mm_s(u, 0)
-                sq(u, 0)
+            widen(0, 0, "s", (0,))
+            widen(0, 1, "v", (0,))
+            widen(0, 1, "v", (1,))
+            widen(0, 1, "s", (2,))
             ss_inter_t(1)
-            widen(1, 0, "v", (2, 3))
+            x_copy(0, 1, "s")
+            ss_inter_t(0)
+            widen(1, 0, "s", (1,))
+            pa_rows()
+            widen(1, 0, "s", (0,))
             quant_t(1)
-            for u in range(2, 4):
-                mm_s(u, 0)
-                sq(u, 0)
-            ss_inter(1, 0)
-            widen(0, 1, "v", (0, 1))
-            quant("s1g0")
-            for u in range(4):
-                mm_s(u, 1)
-                sq(u, 1)
-            ln(0)
-            ln(1)
-            ln(2)
-            widen(0, 1, "v", (2, 3))
-            ss_inter(0, 1)
-            widen(1, 1, "v")
-            quant("s0g1")
-            ss_inter(1, 1)
-            params_a()
-            delta(0)
-            quant("s1g1")
-            mm_s(4, 0)
-            sq(4, 0)
-            ln(3)
-            delta(1)
-            n0_inter(0)
-            delta(2)
-            quant("n0t0")
-            mm_s(4, 1)
-            sq(4, 1)
-            s_unit(5)
-            ln(4)
-            s_unit(6)
-            ln(5)
+            quant_t(0)
+            widen(1, 0, "s", (3,))
+            quant("x0")
+            pa_turn()
+            widen(1, 0, "s", (2,))
+            widen(1, 1, "v", (2,))
+            widen(1, 1, "v", (3,))
+            mm_s(0, 0)
+            pa_out()
             params_b()
+            ss_inter(1, 0)
+            mm_s(1, 0)
+            sq(0, 0)
+            mm_s(2, 0)
+            sq(1, 0)
+            mm_s(3, 0)
+            widen(1, 1, "v", (0,))
+            sq(2, 0)
+            quant("s1g0")
+            sq(3, 0)
+            widen(1, 1, "v", (1,))
             params_c()
-            cs_inter(0)
-            delta(3)
-            quant("c1g0")
-            for i2 in range(2):
-                x_transpose(1, i2)
-                x_copy(1, i2, "v")
-            n0_inter(1)
-            quant("x1")
+            widen(0, 1, "v", (3,))
+            mm_s(0, 1)
+            mm_s(1, 1)
             params_d()
-            delta(4)
-            quant("n0t1")
-            s_unit(7)
-            ln(6)
-            ln(7)
-            delta(5)
-            cs_inter(1)
-            delta(6)
-            delta(7)
-            quant("c1g1")
-            for u in b1:
-                sig(u)
-            LEAD = 3
-            def blend(us, s_us, lead, d_at, dv=False, pend=[]):
-                n = len(us)
-                d_at = dict(d_at)
-                sdone = 0
-                for j in range(n + 3):
-                    if j < n:
-                        mm_q(us[j])
-                    if lead <= j < lead + len(s_us):
-                        s_unit(s_us[j - lead])
-                    if lead + 1 <= j < lead + 1 + len(s_us):
-                        ln(s_us[j - lead - 1])
-                    for u in d_at.get(j, ()):
-                        delta(u)
-                    if j < n:
-                        wd(us[j])
-                    if j >= 3 and UNITS[us[j - 3]][2] == 3:
-                        h, gg, t = UNITS[us[j - 3]]
-                        mul(h, gg, 0, 1)
-                    if 1 <= j <= n:
-                        sub(us[j - 1])
-                        zf(us[j - 1])
-                        if dv and 1 <= j <= 8:
-                            dv_piece((j - 1) // 4, (j - 1) % 4)
-                    if j >= 3 and UNITS[us[j - 3]][2] == 3:
-                        pquant(h, gg, 0, 1)
-                for j in range(len(s_us)):
-                    pass
-            mm_s(8, 0)
-            mm_s(8, 1)
-            mm_s(9, 0)
-            blend(b1, b2, 3, {7: [8], 8: [9], 9: [10], 10: [11, 12]}, True)
-            quant("dvg0")
+            ss_inter(1, 1)
+            mm_s(2, 1)
+            sq(0, 1)
+            sq(1, 1)
+            dv_piece(0, 0)
+            mm_s(3, 1)
+            ln(0)
+            ss_inter(0, 1)
+            dv_piece(0, 1)
+            x_transpose(1, 0)
+            dv_piece(1, 3)
+            ln(1)
+            quant("s1g1")
+            dv_piece(1, 1)
+            quant("s0g1")
+            sq(2, 1)
+            dv_piece(0, 2)
+            delta(1)
+            sq(3, 1)
+            x_copy(1, 0, "v")
+            mm_s(4, 0)
+            dv_piece(1, 0)
+            ln(2)
+            delta(0)
+            mm_s(4, 1)
+            dv_piece(0, 3)
+            x_transpose(1, 1)
+            n0_inter(0)
+            sq(4, 0)
+            dv_piece(1, 2)
+            ln(3)
+            mm_s(5, 0)
+            delta(2)
+            sq(4, 1)
+            x_copy(1, 1, "v")
+            sq(5, 0)
+            delta(3)
+            mm_s(5, 1)
+            ln(4)
             quant("dvg1")
-            for u in b2:
-                sig(u)
+            mm_s(6, 0)
+            mm_s(6, 1)
+            quant("x1")
+            sq(5, 1)
+            quant("dvg0")
+            sq(6, 0)
+            delta(4)
+            mm_s(7, 0)
+            sq(6, 1)
+            n0_inter(1)
+            mm_s(7, 1)
+            sq(7, 0)
+            mm_s(8, 0)
+            ln(5)
+            mm_s(8, 1)
+            cs_inter(0)
+            ln(6)
+            delta(5)
+            sq(7, 1)
+            quant("c1g0")
+            sq(8, 0)
+            delta(6)
+            mm_s(9, 0)
+            sq(8, 1)
+            quant("n0t1")
+            mm_s(9, 1)
+            ln(7)
+            quant("n0t0")
+            mm_s(10, 0)
+            cs_inter(1)
+            sig(0)
+            mm_d(0)
+            delta(7)
+            mm_n(0)
+            mm_d(1)
+            quant("c1g1")
+            mm_n(1)
+            sig(1)
+            mm_d(2)
+            wd(0)
+            sig(2)
+            wd(1)
+            sig(3)
+            mm_n(2)
+            wd(2)
+            sig(4)
+            sub(0)
+            sig(5)
+            sub(1)
+            sig(6)
+            zf(0, "g")
+            mm_d(3)
+            sub(2)
+            sq(9, 0)
+            zf(1, "g")
+            sq(9, 1)
+            mm_n(3)
+            wd(3)
+            zf(2, "g")
+            sq(10, 0)
+            mm_d(4)
+            sig(7)
+            sub(3)
+            ln(8)
+            mm_n(4)
+            mm_d(5)
+            wd(4)
+            zf(3, "g")
+            mm_n(5)
+            mm_s(10, 1)
+            wd(5)
+            mm_s(11, 0)
+            mm_d(6)
+            sub(4)
+            mm_n(6)
+            mul(0, 0, 0, 1)
+            mm_s(11, 1)
+            sq(10, 1)
+            zf(4, "g")
+            mm_d(7)
+            sq(11, 0)
+            mm_n(7)
+            mm_s(12, 0)
+            sq(11, 1)
+            mm_s(12, 1)
+            sq(12, 0)
+            wd(6)
+            sq(12, 1)
+            pquant(0, 0, 0, 1)
+            ln(9)
+            delta(8)
+            wd(7)
+            ln(10)
             mm_s(13, 0)
+            sub(5)
             mm_s(13, 1)
+            sub(6)
+            ln(11)
+            zf(5, "g")
+            mm_d(8)
+            delta(10)
+            mm_n(8)
+            mm_d(9)
+            zf(6, "v")
+            ln(12)
+            sub(7)
+            mm_n(9)
+            delta(9)
+            zf(7, "g")
+            mm_d(10)
+            sig(8)
+            delta(11)
             mm_s(14, 0)
-            blend(b2, b3, 0, {5: [13], 6: [14], 7: [15]})
-            for u in b3:
-                sig(u)
-            for j, u in enumerate(b3 + [None]):
-                if u is not None:
-                    mm_q(u)
-                out_tile(0, j, "s")
-                if u is not None:
-                    wd(u)
-                if j:
-                    sub(b3[j - 1])
-                    zf(b3[j - 1])
-            for i in range(T):
-                mm_o(1, i, 0)
-            for part in range(2):
-                mul(1, 1, part, 2)
-                pquant(1, 1, part, 2)
-            for i in range(T):
-                mm_o(1, i, 1)
-                o_copy(1, i, "sssv"[i])
+            delta(12)
+            mul(0, 1, 0, 1)
+            sig(9)
+            sq(13, 0)
+            sq(13, 1)
+            wd(8)
+            mm_s(14, 1)
+            sq(14, 0)
+            wd(9)
+            mm_s(15, 0)
+            sig(10)
+            sub(8)
+            mm_n(10)
+            sig(11)
+            mm_s(15, 1)
+            pquant(0, 1, 0, 1)
+            zf(8, "g")
+            mm_d(11)
+            sig(12)
+            wd(10)
+            mm_n(11)
+            ln(13)
+            sub(9)
+            wd(11)
+            zf(9, "g")
+            mm_d(12)
+            sub(10)
+            mm_n(12)
+            sub(11)
+            zf(10, "g")
+            mm_d(13)
+            wd(12)
+            sq(14, 1)
+            mm_n(13)
+            mm_d(14)
+            delta(13)
+            sq(15, 0)
+            mm_n(14)
+            sub(12)
+            sq(15, 1)
+            mm_o(0, 0, 0)
+            mm_o(0, 0, 1)
+            zf(11, "v")
+            ln(14)
+            mm_o(0, 1, 0)
+            zf(12, "v")
+            mm_d(15)
+            mul(1, 0, 0, 1)
+            mm_o(0, 1, 1)
+            ln(15)
+            mm_o(0, 2, 0)
+            mm_o(0, 2, 1)
+            sig(13)
+            delta(14)
+            pquant(1, 0, 0, 1)
+            delta(15)
+            sig(14)
+            wd(13)
+            sig(15)
+            wd(14)
+            o_copy(0, 1, "s")
+            mm_n(15)
+            sub(13)
+            o_copy(0, 0, "s")
+            wd(15)
+            o_copy(0, 2, "s")
+            zf(13, "g")
+            sub(14)
+            mm_o(0, 3, 0)
+            mm_o(0, 3, 1)
+            sub(15)
+            zf(14, "g")
+            mm_o(1, 0, 0)
+            zf(15, "v")
+            o_copy(0, 3, "s")
+            mm_o(1, 1, 0)
+            mul(1, 1, 0, 4)
+            mm_o(1, 2, 0)
+            mul(1, 1, 1, 4)
+            pquant(1, 1, 0, 4)
+            mul(1, 1, 2, 4)
+            mm_o(1, 0, 1)
+            pquant(1, 1, 1, 4)
+            mul(1, 1, 3, 4)
+            o_copy(1, 0, "s")
+            mm_o(1, 1, 1)
+            pquant(1, 1, 2, 4)
+            pquant(1, 1, 3, 4)
+            o_copy(1, 1, "s")
+            mm_o(1, 2, 1)
+            mm_o(1, 3, 0)
+            mm_o(1, 3, 1)
+            o_copy(1, 2, "v")
+            o_copy(1, 3, "s")

@@ -16,594 +16,427 @@ ALU = mybir.AluOpType
 ACT = mybir.ActivationFunctionType
 
 P = 128
-T = 4
-H = 512
-UNITS = [(h, g, t) for h in range(2) for g in range(2) for t in range(T)]
-S_BANKS = 3
+PACK = 4
+PASS = P * PACK
+RUN = 8
+
+UNITS = [(h, g, t) for h in range(2) for g in range(2) for t in range(PACK)]
+FIRST_BATCH = 10
 
 
 def tile_learnedstencilwenostep_kernel(tc, x, cs, ss_bytes, ss_scale, gamma, g, dv, out):
     nc = tc.nc
     gain = g
+
     with ExitStack() as ctx:
         keep = ctx.enter_context(tc.tile_pool(name="keep", bufs=1))
         stage = ctx.enter_context(tc.tile_pool(name="stage", bufs=3))
-        psum_s = ctx.enter_context(tc.psum_pool(name="psum_s", bufs=S_BANKS))
-        psum_q = ctx.enter_context(tc.psum_pool(name="psum_q", bufs=8 - S_BANKS))
+        psum_s = ctx.enter_context(tc.psum_pool(name="psum_s", bufs=3))
+        psum_q = ctx.enter_context(tc.psum_pool(name="psum_q", bufs=5))
 
         ident = keep.tile([P, P], F32, name="ident")
         warm = keep.tile([P, 1], F32, name="warm")
-        rows = keep.tile([P, H], BF16, name="rows")
-        rows32 = keep.tile([P, T, P], F32, name="rows32")
-        prm = keep.tile([P, 6, T], F32, name="prm")
-        lng = keep.tile([P, 4, T], F32, name="lng")
-        cbias = keep.tile([P, 2, T], F32, name="cbias")
-        ghalf = keep.tile([P, 2, T], F32, name="ghalf")
-        sc = keep.tile([P, T], F32, name="sc")
-        x_raw = [keep.tile([P, T, D], BF16, name=f"x_raw{h}") for h in range(2)]
-        ss_raw = [keep.tile([P, T, F], U8, name=f"ss_raw{k}") for k in range(2)]
-        cs_raw = [keep.tile([P, T, F], BF16, name=f"cs_raw{k}") for k in range(2)]
-        dv_raw = keep.tile([P, 2, T, D], BF16, name="dv_raw")
-        names = ["x0", "x1", "s0g0", "s0g1", "s1g0", "s1g1", "n0t0", "n0t1", "c1g0", "c1g1", "dvg0", "dvg1"]
-        names += [f"pg{h}{gg}" for h in range(2) for gg in range(2)]
-        codes = {n: keep.tile([P, H], U32, name="codes_" + n, align_bytes=64) for n in names}
-        scales = {n: keep.tile([P, H], U8, name="scales_" + n, align_bytes=64) for n in names}
-        dl = [keep.tile([P, H], F32, name=f"dl{u}") for u in range(16)]
+        rows = keep.tile([P, PASS], BF16, name="rows")
+        rows_by_tile = keep.tile([P, PACK, P], F32, name="rows_by_tile")
+        columns = keep.tile([P, 6, PACK], F32, name="columns")
+        log_gamma = keep.tile([P, 4, PACK], F32, name="log_gamma")
+        log_ratio = keep.tile([P, 2, PACK], F32, name="log_ratio")
+        half_gain = keep.tile([P, 2, PACK], F32, name="half_gain")
+        byte_scale = keep.tile([P, PACK], F32, name="byte_scale")
 
-        nident = keep.tile([P, P], F32, name="nident")
+        x_raw = [keep.tile([P, PACK, D], BF16, name=f"x_raw{h}") for h in range(2)]
+        ss_raw = [keep.tile([P, PACK, F], U8, name=f"ss_raw{k}") for k in range(2)]
+        cs_raw = [keep.tile([P, PACK, F], BF16, name=f"cs_raw{k}") for k in range(2)]
+        dv_raw = keep.tile([P, 2, PACK, D], BF16, name="dv_raw")
+
+        operands = ["x0", "x1", "s0g0", "s0g1", "s1g0", "s1g1", "c1g0", "c1g1", "n0t0", "n0t1", "dvg0", "dvg1"]
+        operands += [f"pg{h}{gg}" for h in range(2) for gg in range(2)]
+        codes = {n: keep.tile([P, PASS], U32, name="codes_" + n, align_bytes=64) for n in operands}
+        scales = {n: keep.tile([P, PASS], U8, name="scales_" + n, align_bytes=64) for n in operands}
+        weight = [keep.tile([P, PASS], F32, name=f"weight{u}") for u in range(len(UNITS))]
+
         make_identity(nc, ident[:])
-        nc.gpsimd.tensor_scalar(out=nident[:], in0=ident[:], scalar1=-1.0, scalar2=0.0, op0=ALU.mult, op1=ALU.add)
         nc.gpsimd.memset(rows[:], 0.0)
         nc.vector.memset(warm[:], 1.0)
 
-        nc.sync.dma_start(out=sc[:], in_=ss_scale.rearrange("o (p j) q -> p (o j q)", j=T))
-        x_half = x[0:H, :].rearrange("(r i) k -> r i k", i=T)
-        nc.sync.dma_start(out=x_raw[0][:, 0:2, :], in_=x_half[:, 0:2, :])
-        nc.sync.dma_start(out=ss_raw[0][:], in_=ss_bytes[0].rearrange("(p j) f -> p j f", j=T))
-        nc.sync.dma_start(out=x_raw[0][:, 2:4, :], in_=x_half[:, 2:4, :])
-        nc.sync.dma_start(out=ss_raw[1][:], in_=ss_bytes[1].rearrange("(p j) f -> p j f", j=T))
-        nc.sync.dma_start(out=rows[0:4, :], in_=gamma.rearrange("v (g f) -> (v g) f", g=2))
+        x_view = x.rearrange("(h r i) k -> h r i k", h=2, i=PACK)
+        nc.sync.dma_start(out=byte_scale[:], in_=ss_scale.rearrange("o (p j) q -> p (o j q)", j=PACK))
+        nc.sync.dma_start(out=ss_raw[0][:], in_=ss_bytes[0].rearrange("(p j) f -> p j f", j=PACK))
+        for i in (0, 2):
+            nc.sync.dma_start(out=x_raw[0][:, i : i + 2, :], in_=x_view[0, :, i : i + 2, :])
+        nc.sync.dma_start(out=ss_raw[1][:], in_=ss_bytes[1].rearrange("(p j) f -> p j f", j=PACK))
+        nc.sync.dma_start(out=rows[0:4, :], in_=gamma.rearrange("k (g f) -> (k g) f", g=2))
         nc.sync.dma_start(out=rows[4:6, :], in_=gain.rearrange("(g f) -> g f", g=2))
         for k in range(2):
-            nc.sync.dma_start(out=cs_raw[k][:], in_=cs[k].rearrange("(p j) f -> p j f", j=T))
-        nc.sync.dma_start(out=x_raw[1][:], in_=x[H:B, :].rearrange("(r i) k -> r i k", i=T))
-        dv_view = dv.rearrange("(g a t b) n -> g t a b n", g=2, t=T, b=8)
+            nc.sync.dma_start(out=cs_raw[k][:], in_=cs[k].rearrange("(p j) f -> p j f", j=PACK))
+        nc.sync.dma_start(out=x_raw[1][:], in_=x_view[1])
+        dv_view = dv.rearrange("(g a t b) n -> g t a b n", g=2, t=PACK, b=RUN)
         for gg in range(2):
-            for t in range(T):
+            for t in range(PACK):
                 nc.sync.dma_start(out=dv_raw[:, gg, t, :], in_=dv_view[gg, t])
 
-        def grouped_tile():
-            return stage.tile([P, 4 * H], BF16, name="grouped", tag="grouped", bufs=6, align_bytes=64)
+        packed = {}
 
-        grouped = {}
+        def packed_tile(n):
+            if n not in packed:
+                packed[n] = stage.tile([P, PACK * PASS], BF16, name="packed", tag="packed", bufs=6, align_bytes=64)
+            return packed[n]
 
-        def quant(n):
-            nc.vector.quantize_mx(out=codes[n][:].bitcast(FP8X4), scales=scales[n][:], in_=grouped[n][:])
+        def quantise(n, lo=0, hi=PASS):
+            nc.vector.quantize_mx(
+                out=codes[n][:, lo:hi].bitcast(FP8X4),
+                scales=scales[n][:, lo:hi],
+                in_=packed[n][:, PACK * lo : PACK * hi],
+            )
 
-        def mm(acc, l, lcols, r, start, stop, tok=slice(0, H)):
+        def multiply(acc, stationary, column, moving, start, stop):
+            cols = slice(column, column + P)
             nc.tensor.matmul_mx(
                 out=acc,
-                lhsT=codes[l][:, lcols].bitcast(FP8X4), lhsT_scale=scales[l][:, lcols],
-                rhs=codes[r][:, tok].bitcast(FP8X4), rhs_scale=scales[r][:, tok],
-                start=start, stop=stop,
+                lhsT=codes[stationary][:, cols].bitcast(FP8X4),
+                lhsT_scale=scales[stationary][:, cols],
+                rhs=codes[moving][:].bitcast(FP8X4),
+                rhs_scale=scales[moving][:],
+                start=start,
+                stop=stop,
             )
 
-        xbank = {}
+        turned = {}
 
-        def x_transpose(h, i2):
-            bank = psum_s.tile([P, 2, 2, P], F32, name="ps", tag="ps")
+        def turn_tokens(h, pair):
+            bank = psum_s.tile([P, 2, 2, P], F32, name="s_bank", tag="s_bank")
             for i in range(2):
-                words = x_raw[h][:, 2 * i2 + i, :].bitcast(F32)
+                words = x_raw[h][:, 2 * pair + i, :].bitcast(F32)
                 for w in range(2):
                     nc.tensor.transpose(bank[:, i, w, :], words[:, w::2], ident[:])
-            xbank[h, i2] = bank
+            turned[h, pair] = bank
 
-        def x_copy(h, i2, engine):
-            n = f"x{h}"
-            if n not in grouped:
-                grouped[n] = grouped_tile()
-            dst = grouped[n][:].bitcast(F32)[:, i2 * H : (i2 + 1) * H]
-            copy = nc.scalar.copy if engine == "s" else nc.vector.tensor_copy
-            copy(out=dst.rearrange("p (i r w) -> p i r w", i=2, w=2), in_=xbank[h, i2][:].rearrange("p i w r -> p i r w"))
+        def pack_tokens(h, pair, copy):
+            dst = packed_tile(f"x{h}")[:].bitcast(F32)[:, pair * PASS : (pair + 1) * PASS]
+            copy(
+                out=dst.rearrange("p (i r w) -> p i r w", i=2, w=2),
+                in_=turned[h, pair][:].rearrange("p i w r -> p i r w"),
+            )
 
-        wide = {}
+        widened = {}
 
-        def widen(k, gg, engine, js=range(T)):
-            if (k, gg) not in wide:
-                wide[k, gg] = stage.tile([P, T, H], BF16, name="wide", tag="wide", bufs=3)
-            wt = wide[k, gg]
+        def widen(k, gg, js, engine):
+            if (k, gg) not in widened:
+                widened[k, gg] = stage.tile([P, PACK, PASS], BF16, name="wide", tag="wide", bufs=3)
             for j in js:
-                src = ss_raw[k][:, j, gg * H : (gg + 1) * H].bitcast(FP8)
-                if engine == "s":
-                    nc.scalar.activation(out=wt[:, j, :], in_=src, func=ACT.Copy, scale=sc[:, j : j + 1])
+                dst = widened[k, gg][:, j, :]
+                src = ss_raw[k][:, j, gg * PASS : (gg + 1) * PASS].bitcast(FP8)
+                scale = byte_scale[:, j : j + 1]
+                if engine == "scalar":
+                    nc.scalar.activation(out=dst, in_=src, func=ACT.Copy, scale=scale)
                 else:
-                    nc.vector.tensor_scalar(out=wt[:, j, :], in0=src, scalar1=sc[:, j : j + 1], scalar2=None, op0=ALU.mult)
+                    nc.vector.tensor_scalar(out=dst, in0=src, scalar1=scale, scalar2=None, op0=ALU.mult)
 
-        def interleave(n, src):
-            gt = grouped_tile()
-            grouped[n] = gt
+        def by_tile(ap):
+            return ap.rearrange("p j (a t b) -> p t a j b", t=PACK, b=RUN)
+
+        def packed_by_tile(ap):
+            return ap.rearrange("p (t a b j) -> p t a j b", a=P // RUN, b=RUN, j=PACK)
+
+        def pack_ss(k, gg, tiles=slice(0, PACK)):
+            n = f"s{k}g{gg}"
+            nc.vector.tensor_copy(out=packed_by_tile(packed_tile(n)[:])[:, tiles], in_=by_tile(widened[k, gg][:])[:, tiles])
+
+        def pack_c1(gg):
             nc.vector.tensor_copy(
-                out=gt[:].rearrange("p (t a b j) -> p t a j b", t=T, b=8, j=T),
-                in_=src.rearrange("p j (a t b) -> p t a j b", t=T, b=8),
+                out=packed_by_tile(packed_tile(f"c1g{gg}")[:]),
+                in_=by_tile(cs_raw[1][:, :, gg * PASS : (gg + 1) * PASS]),
             )
 
-        def ss_inter(k, gg):
-            interleave(f"s{k}g{gg}", wide[k, gg][:])
-
-        def ss_inter_t(t2):
-            if "s0g0" not in grouped:
-                grouped["s0g0"] = grouped_tile()
-            lo = t2 * 2
-            nc.vector.tensor_copy(
-                out=grouped["s0g0"][:].rearrange("p (t a b j) -> p t a j b", t=T, b=8, j=T)[:, lo : lo + 2],
-                in_=wide[0, 0][:].rearrange("p j (a t b) -> p t a j b", t=T, b=8)[:, lo : lo + 2],
-            )
-
-        def quant_t(t2):
-            lo = t2 * 2 * P
-            nc.vector.quantize_mx(
-                out=codes["s0g0"][:, lo : lo + 2 * P].bitcast(FP8X4), scales=scales["s0g0"][:, lo : lo + 2 * P],
-                in_=grouped["s0g0"][:, 4 * lo : 4 * (lo + 2 * P)],
-            )
-
-        def cs_inter(gg):
-            interleave(f"c1g{gg}", cs_raw[1][:, :, gg * H : (gg + 1) * H])
-
-        def n0_inter(t2):
-            gt = grouped_tile()
-            grouped[f"n0t{t2}"] = gt
-            s5 = cs_raw[0][:].rearrange("p j (a t b) -> p t a j b", t=T, b=8)
-            d5 = gt[:].rearrange("p (t a b j) -> p t a j b", t=2, b=8, j=T)
+        def pack_n0(pair):
+            src = by_tile(cs_raw[0][:])
+            dst = packed_tile(f"n0t{pair}")[:].rearrange("p (t a b j) -> p t a j b", t=2, b=RUN, j=PACK)
             for t in range(2):
-                nc.vector.tensor_scalar(out=d5[:, t], in0=s5[:, 2 * t2 + t], scalar1=-1.0, scalar2=None, op0=ALU.mult)
+                nc.vector.tensor_scalar(out=dst[:, t], in0=src[:, 2 * pair + t], scalar1=-1.0, scalar2=None, op0=ALU.mult)
 
-        def dv_inter(gg):
-            n = f"dvg{gg}"
-            gt = grouped_tile()
-            grouped[n] = gt
-            return gt
-
-        def dv_piece(gg, q):
-            if f"dvg{gg}" not in grouped:
-                dv_inter(gg)
-            w = D // 4
-            nc.gpsimd.tensor_scalar(
-                out=grouped[f"dvg{gg}"][:, 4 * q * w : 4 * (q + 1) * w].rearrange("p (c i t) -> p c t i", i=8, t=T),
-                in0=dv_raw[:, gg, :, q * w : (q + 1) * w].rearrange("p t (c i) -> p c t i", i=8),
-                scalar1=1.0, scalar2=0.0, op0=ALU.mult, op1=ALU.add,
+        def pack_dv(gg):
+            nc.vector.tensor_copy(
+                out=packed_tile(f"dvg{gg}")[:].rearrange("p (c i t) -> p c t i", i=RUN, t=PACK),
+                in_=dv_raw[:, gg].rearrange("p t (c i) -> p c t i", i=RUN),
             )
 
-        sbank = {}
-        dbk = {}
-        ul = {}
+        def sort_rows():
+            nc.gpsimd.tensor_scalar(
+                out=rows_by_tile[:].rearrange("p t (a b) -> p t a b", b=RUN),
+                in0=rows[:].rearrange("p (a t b) -> p t a b", t=PACK, b=RUN),
+                scalar1=1.0,
+                scalar2=0.0,
+                op0=ALU.mult,
+                op1=ALU.add,
+            )
 
-        def mm_s(u, k):
+        def turn_rows():
+            bank = psum_s.tile([P, PACK, P], F32, name="s_bank", tag="s_bank")
+            for t in range(PACK):
+                nc.tensor.transpose(bank[:, t, :], rows_by_tile[:, t, :], ident[:])
+            nc.scalar.copy(out=columns[:], in_=bank[:, :, 0:6].rearrange("p t r -> p r t"))
+
+        def clamp_gamma():
+            nc.vector.tensor_scalar(out=log_gamma[:], in0=columns[:, 0:4, :], scalar1=2.0**-64, scalar2=None, op0=ALU.max)
+            nc.vector.tensor_scalar(out=half_gain[:], in0=columns[:, 4:6, :], scalar1=0.5, scalar2=None, op0=ALU.mult)
+
+        s_bank = {}
+        logs = {}
+
+        def indicator(u, k):
             h, gg, t = UNITS[u]
-            acc = psum_s.tile([P, H], F32, name="ps", tag="ps")
-            sbank[u, k] = acc
-            mm(acc[:], f"s{k}g{gg}", slice(t * P, (t + 1) * P), f"x{h}", True, True)
+            s_bank[u, k] = psum_s.tile([P, PASS], F32, name="s_bank", tag="s_bank")
+            multiply(s_bank[u, k][:], f"s{k}g{gg}", t * P, f"x{h}", True, True)
 
-        def sq(u, k):
-            if k == 0:
-                ul[u] = stage.tile([P, 2, H], F32, name="ul", tag="ul", bufs=5)
-            nc.scalar.activation(out=ul[u][:, k, :], in_=sbank[u, k][:], func=ACT.Square)
+        def square(u, k):
+            if u not in logs:
+                logs[u] = stage.tile([P, 2, PASS], F32, name="logs", tag="logs", bufs=5)
+            nc.scalar.activation(out=logs[u][:, k, :], in_=s_bank[u, k][:], func=ACT.Square)
 
-        def ln(u):
-            nc.scalar.activation(out=ul[u][:], in_=ul[u][:], func=ACT.Ln, bias=0.5, scale=1.0)
+        def log(u):
+            nc.scalar.activation(out=logs[u][:], in_=logs[u][:], func=ACT.Ln, bias=0.5, scale=1.0)
 
-        def delta(u):
-            nc.vector.tensor_tensor(out=dl[u][:], in0=ul[u][:, 0, :], in1=ul[u][:, 1, :], op=ALU.subtract)
+        def log_difference(u):
+            nc.vector.tensor_tensor(out=weight[u][:], in0=logs[u][:, 0, :], in1=logs[u][:, 1, :], op=ALU.subtract)
 
-        def pdelta(u):
-            bank = psum_s.tile([P, H], F32, name="ps", tag="ps")
-            nc.tensor.matmul(bank[:], lhsT=ident[:], rhs=ul[u][:, 0, :], start=True, stop=False)
-            nc.tensor.matmul(bank[:], lhsT=nident[:], rhs=ul[u][:, 1, :], start=False, stop=True)
-            dbk[u] = bank
-
-        def sig(u):
+        def sigmoid(u):
             h, gg, t = UNITS[u]
-            nc.scalar.activation(out=dl[u][:], in_=dbk[u][:] if u in dbk else dl[u][:], func=ACT.Sigmoid, bias=cbias[:, gg, t : t + 1], scale=2.0)
+            nc.scalar.activation(
+                out=weight[u][:], in_=weight[u][:], func=ACT.Sigmoid, bias=log_ratio[:, gg, t : t + 1], scale=2.0
+            )
 
-        nbank, dbank, mt, qh, zz = {}, {}, {}, {}, {}
+        def squared(u, k):
+            indicator(u, k)
+            square(u, k)
 
-        def q_operands(u):
+        difference, minus_q0, step, blend, lifted = {}, {}, {}, {}, {}
+
+        def candidates(u):
             h, gg, t = UNITS[u]
-            cols = slice(t * P, (t + 1) * P)
-            n0 = t % 2 * 2 + gg
-            return f"c1g{gg}", cols, f"n0t{t // 2}", slice(n0 * P, (n0 + 1) * P), f"x{h}"
+            n0, n0_column = f"n0t{t // 2}", (t % 2 * 2 + gg) * P
+            difference[u] = psum_q.tile([P, PASS], F32, name="q_bank", tag="q_bank")
+            multiply(difference[u][:], f"c1g{gg}", t * P, f"x{h}", True, False)
+            multiply(difference[u][:], n0, n0_column, f"x{h}", False, True)
+            minus_q0[u] = psum_q.tile([P, PASS], F32, name="q_bank", tag="q_bank")
+            multiply(minus_q0[u][:], n0, n0_column, f"x{h}", True, True)
 
-        def mm_d(u):
-            c1, cols, n0, ncols, xx = q_operands(u)
-            dbank[u] = psum_q.tile([P, H], F32, name="pq", tag="pq")
-            mm(dbank[u][:], c1, cols, xx, True, False)
-            mm(dbank[u][:], n0, ncols, xx, False, True)
+        def weigh(u):
+            step[u] = stage.tile([P, PASS], F32, name="step", tag="step", bufs=3)
+            nc.vector.tensor_tensor(out=step[u][:], in0=difference[u][:], in1=weight[u][:], op=ALU.mult)
 
-        def mm_n(u):
-            c1, cols, n0, ncols, xx = q_operands(u)
-            nbank[u] = psum_q.tile([P, H], F32, name="pq", tag="pq")
-            mm(nbank[u][:], n0, ncols, xx, True, True)
-
-        def wd(u):
-            mt[u] = stage.tile([P, H], F32, name="mt", tag="mt", bufs=3)
-            nc.vector.tensor_tensor(out=mt[u][:], in0=dbank[u][:], in1=dl[u][:], op=ALU.mult)
-
-        def sub(u):
+        def blend_and_lift(u, engine):
             h, gg, t = UNITS[u]
-            if (h, gg) not in qh:
-                qh[h, gg] = stage.tile([P, T, H], F32, name="qh", tag="qh", bufs=2)
-                zz[h, gg] = stage.tile([P, T, H], F32, name="zz", tag="zz", bufs=2)
-            nc.vector.tensor_tensor(out=qh[h, gg][:, t, :], in0=mt[u][:], in1=nbank[u][:], op=ALU.subtract)
+            if (h, gg) not in blend:
+                blend[h, gg] = stage.tile([P, PACK, PASS], F32, name="blend", tag="blend", bufs=2)
+                lifted[h, gg] = stage.tile([P, PACK, PASS], F32, name="lifted", tag="lifted", bufs=2)
+            nc.vector.tensor_tensor(out=blend[h, gg][:, t, :], in0=step[u][:], in1=minus_q0[u][:], op=ALU.subtract)
+            if engine is not None:
+                lift(u, engine)
 
-        def zf(u, engine):
+        def lift(u, engine):
             h, gg, t = UNITS[u]
-            half, full = ghalf[:, gg, t : t + 1], prm[:, 4 + gg, t : t + 1]
-            dst, src = zz[h, gg][:, t, :], qh[h, gg][:, t, :]
-            if engine == "s":
-                nc.scalar.activation(out=dst, in_=src, func=ACT.Identity, scale=half, bias=full)
+            dst, src = lifted[h, gg][:, t, :], blend[h, gg][:, t, :]
+            half, whole = half_gain[:, gg, t : t + 1], columns[:, 4 + gg, t : t + 1]
+            if engine == "scalar":
+                nc.scalar.activation(out=dst, in_=src, func=ACT.Identity, scale=half, bias=whole)
             else:
-                e = nc.vector if engine == "v" else nc.gpsimd
-                e.tensor_scalar(out=dst, in0=src, scalar1=half, scalar2=full, op0=ALU.mult, op1=ALU.add)
+                (nc.gpsimd if engine == "gpsimd" else nc.vector).tensor_scalar(out=dst, in0=src, scalar1=half, scalar2=whole, op0=ALU.mult, op1=ALU.add)
 
-        def mul(h, gg, part, parts):
-            n = f"pg{h}{gg}"
-            if n not in grouped:
-                grouped[n] = grouped_tile()
-            w = H // parts
-            lo = part * w
+        def pack_pg(h, gg, lo=0, hi=PASS):
             nc.vector.tensor_tensor(
-                out=grouped[n][:, 4 * lo : 4 * (lo + w)].rearrange("p (c i t) -> p c t i", i=4, t=T),
-                in0=zz[h, gg][:, :, lo : lo + w].rearrange("p t (c i) -> p c t i", i=4),
-                in1=qh[h, gg][:, :, lo : lo + w].rearrange("p t (c i) -> p c t i", i=4),
+                out=packed_tile(f"pg{h}{gg}")[:, PACK * lo : PACK * hi].rearrange("p (c i t) -> p c t i", i=4, t=PACK),
+                in0=lifted[h, gg][:, :, lo:hi].rearrange("p t (c i) -> p c t i", i=4),
+                in1=blend[h, gg][:, :, lo:hi].rearrange("p t (c i) -> p c t i", i=4),
                 op=ALU.mult,
             )
 
-        def pquant(h, gg, part, parts):
-            n = f"pg{h}{gg}"
-            w = H // parts
-            lo = part * w
-            nc.vector.quantize_mx(
-                out=codes[n][:, lo : lo + w].bitcast(FP8X4), scales=scales[n][:, lo : lo + w],
-                in_=grouped[n][:, 4 * lo : 4 * (lo + w)],
-            )
+        out_view = out.rearrange("(h r i) d -> h i r d", h=2, i=PACK)
+        out_bank = {}
 
-        out_view = out.rearrange("(h r i) d -> h i r d", h=2, i=T)
-        obank = {}
-
-        def mm_o(h, i, gg):
+        def divergence(h, i, gg):
             if gg == 0:
-                obank[h, i] = psum_s.tile([P, D], F32, name="ps", tag="ps")
-            mm(obank[h, i][:], f"pg{h}{gg}", slice(i * P, (i + 1) * P), f"dvg{gg}", gg == 0, gg == 1)
+                out_bank[h, i] = psum_s.tile([P, D], F32, name="s_bank", tag="s_bank")
+            multiply(out_bank[h, i][:], f"pg{h}{gg}", i * P, f"dvg{gg}", gg == 0, gg == 1)
 
-        def o_copy(h, i, engine):
-            ot = stage.tile([P, D], F32, name="ot", tag="ot", bufs=4)
-            if engine == "s":
-                nc.scalar.copy(out=ot[:], in_=obank[h, i][:])
-            else:
-                nc.vector.tensor_copy(out=ot[:], in_=obank[h, i][:])
-            nc.sync.dma_start(out=out_view[h, i], in_=ot[:])
-
-        def pa_rows():
-            nc.gpsimd.tensor_scalar(
-                out=rows32[:].rearrange("p t (a b) -> p t a b", b=8), in0=rows[:].rearrange("p (a t b) -> p t a b", t=T, b=8),
-                scalar1=1.0, scalar2=0.0, op0=ALU.mult, op1=ALU.add,
-            )
-
-        pbank = {}
-
-        def pa_turn():
-            bank = psum_s.tile([P, T, P], F32, name="ps", tag="ps")
-            for t in range(T):
-                nc.tensor.transpose(bank[:, t, :], rows32[:, t, :], ident[:])
-            pbank[0] = bank
-
-        def pa_out():
-            nc.scalar.copy(out=prm[:], in_=pbank[0][:, :, 0:6].rearrange("p t r -> p r t"))
-
-        def params_b():
-            nc.vector.tensor_scalar(out=lng[:], in0=prm[:, 0:4, :], scalar1=2.0**-64, scalar2=None, op0=ALU.max)
-            nc.vector.tensor_scalar(out=ghalf[:], in0=prm[:, 4:6, :], scalar1=0.5, scalar2=None, op0=ALU.mult)
-
-        def params_c():
-            nc.scalar.activation(out=lng[:], in_=lng[:], func=ACT.Ln)
-
-        def params_d():
-            nc.vector.tensor_tensor(out=cbias[:], in0=lng[:, 2:4, :], in1=lng[:, 0:2, :], op=ALU.subtract)
-
-
-        def out_tile(h, i, engine):
-            mm_o(h, i, 0)
-            mm_o(h, i, 1)
-            o_copy(h, i, engine)
+        def store(h, i, copy):
+            result = stage.tile([P, D], F32, name="result", tag="result", bufs=4)
+            copy(out=result[:], in_=out_bank[h, i][:])
+            nc.sync.dma_start(out=out_view[h, i], in_=result[:])
 
         with tc.manual_schedule():
             nc.scalar.activation(out=warm[:], in_=warm[:], func=ACT.Ln)
-            x_transpose(0, 0)
-            x_copy(0, 0, "v")
-            widen(0, 0, "v", (1,))
-            widen(0, 0, "s", (3,))
-            widen(0, 0, "v", (2,))
-            x_transpose(0, 1)
-            widen(0, 0, "s", (0,))
-            widen(0, 1, "v", (0,))
-            widen(0, 1, "v", (1,))
-            widen(0, 1, "s", (2,))
-            ss_inter_t(1)
-            x_copy(0, 1, "s")
-            ss_inter_t(0)
-            widen(1, 0, "s", (1,))
-            pa_rows()
-            widen(1, 0, "s", (0,))
-            quant_t(1)
-            quant_t(0)
-            widen(1, 0, "s", (3,))
-            quant("x0")
-            pa_turn()
-            widen(1, 0, "s", (2,))
-            widen(1, 1, "v", (2,))
-            widen(1, 1, "v", (3,))
-            mm_s(0, 0)
-            pa_out()
-            params_b()
-            ss_inter(1, 0)
-            mm_s(1, 0)
-            sq(0, 0)
-            mm_s(2, 0)
-            sq(1, 0)
-            mm_s(3, 0)
-            widen(1, 1, "v", (0,))
-            sq(2, 0)
-            quant("s1g0")
-            sq(3, 0)
-            widen(1, 1, "v", (1,))
-            params_c()
-            widen(0, 1, "v", (3,))
-            mm_s(0, 1)
-            mm_s(1, 1)
-            params_d()
-            ss_inter(1, 1)
-            mm_s(2, 1)
-            sq(0, 1)
-            sq(1, 1)
-            dv_piece(0, 0)
-            mm_s(3, 1)
-            ln(0)
-            ss_inter(0, 1)
-            dv_piece(0, 1)
-            x_transpose(1, 0)
-            dv_piece(1, 3)
-            ln(1)
-            quant("s1g1")
-            dv_piece(1, 1)
-            quant("s0g1")
-            sq(2, 1)
-            dv_piece(0, 2)
-            delta(1)
-            sq(3, 1)
-            x_copy(1, 0, "v")
-            mm_s(4, 0)
-            dv_piece(1, 0)
-            ln(2)
-            delta(0)
-            mm_s(4, 1)
-            dv_piece(0, 3)
-            x_transpose(1, 1)
-            n0_inter(0)
-            sq(4, 0)
-            dv_piece(1, 2)
-            ln(3)
-            mm_s(5, 0)
-            delta(2)
-            sq(4, 1)
-            x_copy(1, 1, "v")
-            sq(5, 0)
-            delta(3)
-            mm_s(5, 1)
-            ln(4)
-            quant("dvg1")
-            mm_s(6, 0)
-            mm_s(6, 1)
-            quant("x1")
-            sq(5, 1)
-            quant("dvg0")
-            sq(6, 0)
-            delta(4)
-            mm_s(7, 0)
-            sq(6, 1)
-            n0_inter(1)
-            mm_s(7, 1)
-            sq(7, 0)
-            mm_s(8, 0)
-            ln(5)
-            mm_s(8, 1)
-            cs_inter(0)
-            ln(6)
-            delta(5)
-            sq(7, 1)
-            quant("c1g0")
-            sq(8, 0)
-            delta(6)
-            mm_s(9, 0)
-            sq(8, 1)
-            quant("n0t1")
-            mm_s(9, 1)
-            ln(7)
-            quant("n0t0")
-            mm_s(10, 0)
-            cs_inter(1)
-            sig(0)
-            mm_d(0)
-            delta(7)
-            mm_n(0)
-            mm_d(1)
-            quant("c1g1")
-            mm_n(1)
-            sig(1)
-            mm_d(2)
-            wd(0)
-            sig(2)
-            wd(1)
-            sig(3)
-            mm_n(2)
-            wd(2)
-            sig(4)
-            sub(0)
-            sig(5)
-            sub(1)
-            sig(6)
-            zf(0, "g")
-            mm_d(3)
-            sub(2)
-            sq(9, 0)
-            zf(1, "g")
-            sq(9, 1)
-            mm_n(3)
-            wd(3)
-            zf(2, "g")
-            sq(10, 0)
-            mm_d(4)
-            sig(7)
-            sub(3)
-            ln(8)
-            mm_n(4)
-            mm_d(5)
-            wd(4)
-            zf(3, "g")
-            mm_n(5)
-            mm_s(10, 1)
-            wd(5)
-            mm_s(11, 0)
-            mm_d(6)
-            sub(4)
-            mm_n(6)
-            mul(0, 0, 0, 1)
-            mm_s(11, 1)
-            sq(10, 1)
-            zf(4, "g")
-            mm_d(7)
-            sq(11, 0)
-            mm_n(7)
-            mm_s(12, 0)
-            sq(11, 1)
-            mm_s(12, 1)
-            sq(12, 0)
-            wd(6)
-            sq(12, 1)
-            pquant(0, 0, 0, 1)
-            ln(9)
-            delta(8)
-            wd(7)
-            ln(10)
-            mm_s(13, 0)
-            sub(5)
-            mm_s(13, 1)
-            sub(6)
-            ln(11)
-            zf(5, "g")
-            mm_d(8)
-            delta(10)
-            mm_n(8)
-            mm_d(9)
-            zf(6, "v")
-            ln(12)
-            sub(7)
-            mm_n(9)
-            delta(9)
-            zf(7, "g")
-            mm_d(10)
-            sig(8)
-            delta(11)
-            mm_s(14, 0)
-            delta(12)
-            mul(0, 1, 0, 1)
-            sig(9)
-            sq(13, 0)
-            sq(13, 1)
-            wd(8)
-            mm_s(14, 1)
-            sq(14, 0)
-            wd(9)
-            mm_s(15, 0)
-            sig(10)
-            sub(8)
-            mm_n(10)
-            sig(11)
-            mm_s(15, 1)
-            pquant(0, 1, 0, 1)
-            zf(8, "g")
-            mm_d(11)
-            sig(12)
-            wd(10)
-            mm_n(11)
-            ln(13)
-            sub(9)
-            wd(11)
-            zf(9, "g")
-            mm_d(12)
-            sub(10)
-            mm_n(12)
-            sub(11)
-            zf(10, "g")
-            mm_d(13)
-            wd(12)
-            sq(14, 1)
-            mm_n(13)
-            mm_d(14)
-            delta(13)
-            sq(15, 0)
-            mm_n(14)
-            sub(12)
-            sq(15, 1)
-            mm_o(0, 0, 0)
-            mm_o(0, 0, 1)
-            zf(11, "v")
-            ln(14)
-            mm_o(0, 1, 0)
-            zf(12, "v")
-            mm_d(15)
-            mul(1, 0, 0, 1)
-            mm_o(0, 1, 1)
-            ln(15)
-            mm_o(0, 2, 0)
-            mm_o(0, 2, 1)
-            sig(13)
-            delta(14)
-            pquant(1, 0, 0, 1)
-            delta(15)
-            sig(14)
-            wd(13)
-            sig(15)
-            wd(14)
-            o_copy(0, 1, "s")
-            mm_n(15)
-            sub(13)
-            o_copy(0, 0, "s")
-            wd(15)
-            o_copy(0, 2, "s")
-            zf(13, "g")
-            sub(14)
-            mm_o(0, 3, 0)
-            mm_o(0, 3, 1)
-            sub(15)
-            zf(14, "g")
-            mm_o(1, 0, 0)
-            zf(15, "v")
-            o_copy(0, 3, "s")
-            mm_o(1, 1, 0)
-            mul(1, 1, 0, 4)
-            mm_o(1, 2, 0)
-            mul(1, 1, 1, 4)
-            pquant(1, 1, 0, 4)
-            mul(1, 1, 2, 4)
-            mm_o(1, 0, 1)
-            pquant(1, 1, 1, 4)
-            mul(1, 1, 3, 4)
-            o_copy(1, 0, "s")
-            mm_o(1, 1, 1)
-            pquant(1, 1, 2, 4)
-            pquant(1, 1, 3, 4)
-            o_copy(1, 1, "s")
-            mm_o(1, 2, 1)
-            mm_o(1, 3, 0)
-            mm_o(1, 3, 1)
-            o_copy(1, 2, "v")
-            o_copy(1, 3, "s")
+
+            widen(0, 0, (0, 1), "vector")
+            widen(0, 0, (2, 3), "scalar")
+            widen(0, 1, (0, 1), "vector")
+            for pair in range(2):
+                turn_tokens(0, pair)
+                pack_tokens(0, pair, nc.scalar.copy)
+            widen(1, 0, (0, 1, 2), "scalar")
+            pack_ss(0, 0, slice(0, 2))
+            pack_ss(0, 0, slice(2, 4))
+            quantise("s0g0", 0, 2 * P)
+            quantise("x0")
+            quantise("s0g0", 2 * P, PASS)
+            widen(1, 0, (3,), "vector")
+            widen(0, 1, (2,), "vector")
+            for u in range(4):
+                squared(u, 0)
+            pack_ss(1, 0)
+            widen(0, 1, (3,), "vector")
+            quantise("s1g0")
+            for u in range(2):
+                squared(u, 1)
+            log(0)
+            log(1)
+            for u in range(2, 4):
+                squared(u, 1)
+            log(2)
+            log(3)
+
+            widen(1, 1, range(PACK), "vector")
+            pack_ss(0, 1)
+            pack_ss(1, 1)
+            quantise("s0g1")
+            quantise("s1g1")
+            turn_tokens(1, 0)
+            turn_tokens(1, 1)
+            pack_tokens(1, 0, nc.vector.tensor_copy)
+            pack_tokens(1, 1, nc.vector.tensor_copy)
+            log_difference(0)
+            quantise("x1")
+            sort_rows()
+            squared(4, 0)
+            squared(4, 1)
+            turn_rows()
+            log(4)
+            log_difference(1)
+            log_difference(2)
+            log_difference(3)
+            clamp_gamma()
+            nc.scalar.activation(out=log_gamma[:], in_=log_gamma[:], func=ACT.Ln)
+
+            pack_n0(0)
+            log_difference(4)
+            pack_n0(1)
+            nc.vector.tensor_tensor(out=log_ratio[:], in0=log_gamma[:, 2:4, :], in1=log_gamma[:, 0:2, :], op=ALU.subtract)
+            pack_c1(0)
+            squared(5, 0)
+            squared(5, 1)
+            for u in range(6, FIRST_BATCH):
+                squared(u, 0)
+                log(u - 1)
+                squared(u, 1)
+            log(FIRST_BATCH - 1)
+            log_difference(5)
+            quantise("n0t0")
+            quantise("n0t1")
+            log_difference(6)
+            pack_c1(1)
+            quantise("c1g0")
+            log_difference(7)
+            quantise("c1g1")
+            pack_dv(0)
+            log_difference(8)
+            pack_dv(1)
+            log_difference(9)
+            quantise("dvg0")
+
+            for u in range(FIRST_BATCH):
+                sigmoid(u)
+            candidates(0)
+            candidates(1)
+            indicator(10, 0)
+            indicator(10, 1)
+            indicator(11, 0)
+            weigh(0)
+            quantise("dvg1")
+            blend_and_lift(0, "gpsimd")
+            candidates(2)
+            weigh(1)
+            weigh(2)
+            blend_and_lift(1, "gpsimd")
+            blend_and_lift(2, "gpsimd")
+            candidates(3)
+            candidates(4)
+            weigh(3)
+            weigh(4)
+            blend_and_lift(3, "gpsimd")
+            blend_and_lift(4, "gpsimd")
+            candidates(5)
+            square(10, 0)
+            square(10, 1)
+            square(11, 0)
+            squared(11, 1)
+            log(10)
+            indicator(12, 0)
+            candidates(6)
+            indicator(12, 1)
+            weigh(5)
+            weigh(6)
+            blend_and_lift(5, "gpsimd")
+            blend_and_lift(6, "gpsimd")
+            square(12, 0)
+            log(11)
+            square(12, 1)
+            squared(13, 0)
+            candidates(7)
+            candidates(8)
+            pack_pg(0, 0)
+            weigh(7)
+            log_difference(10)
+            quantise("pg00")
+            weigh(8)
+            blend_and_lift(7, None)
+            blend_and_lift(8, "gpsimd")
+            lift(7, "vector")
+            log(12)
+            squared(13, 1)
+            squared(14, 0)
+            log(13)
+            candidates(9)
+            squared(14, 1)
+            squared(15, 0)
+            log(14)
+            squared(15, 1)
+            log(15)
+            log_difference(11)
+            log_difference(12)
+            weigh(9)
+            log_difference(13)
+            blend_and_lift(9, "gpsimd")
+            pack_pg(0, 1)
+            log_difference(14)
+            quantise("pg01")
+            log_difference(15)
+
+            for u in range(FIRST_BATCH, len(UNITS)):
+                sigmoid(u)
+            for u in range(FIRST_BATCH, len(UNITS), 2):
+                last = u + 2 == len(UNITS)
+                candidates(u)
+                candidates(u + 1)
+                weigh(u)
+                weigh(u + 1)
+                blend_and_lift(u, "scalar" if last else "gpsimd")
+                blend_and_lift(u + 1, "scalar" if last else "gpsimd")
+                if not last:
+                    for i in (u - FIRST_BATCH, u - FIRST_BATCH + 1):
+                        divergence(0, i, 0)
+                        divergence(0, i, 1)
+                        store(0, i, nc.scalar.copy)
+            pack_pg(1, 0)
+
+            pack_pg(1, 1, 0, P)
+            quantise("pg10")
+            for i in range(3):
+                divergence(1, i, 0)
+            for i in range(1, PACK):
+                pack_pg(1, 1, i * P, (i + 1) * P)
+                quantise("pg11", (i - 1) * P, i * P)
+            quantise("pg11", 3 * P, PASS)
+            for i in range(PACK):
+                if i == 3:
+                    divergence(1, i, 0)
+                divergence(1, i, 1)
+                store(1, i, (nc.scalar.copy, nc.vector.tensor_copy)[i % 2])

@@ -242,8 +242,8 @@ def tile_learnedstencilwenostep_kernel(tc, x, cs, ss_bytes, ss_scale, gamma, g, 
             else:
                 (nc.gpsimd if engine == "gpsimd" else nc.vector).tensor_scalar(out=dst, in0=src, scalar1=half, scalar2=whole, op0=ALU.mult, op1=ALU.add)
 
-        def pack_pg(h, gg, lo=0, hi=PASS):
-            nc.vector.tensor_tensor(
+        def pack_pg(h, gg, lo=0, hi=PASS, multiply=nc.vector.tensor_tensor):
+            multiply(
                 out=packed_tile(f"pg{h}{gg}")[:, PACK * lo : PACK * hi].rearrange("p (c i t) -> p c t i", i=4, t=PACK),
                 in0=lifted[h, gg][:, :, lo:hi].rearrange("p t (c i) -> p c t i", i=4),
                 in1=blend[h, gg][:, :, lo:hi].rearrange("p t (c i) -> p c t i", i=4),
@@ -255,7 +255,10 @@ def tile_learnedstencilwenostep_kernel(tc, x, cs, ss_bytes, ss_scale, gamma, g, 
 
         def divergence(h, i, gg):
             if gg == 0:
-                out_bank[h, i] = psum_s.tile([P, D], F32, name="s_bank", tag="s_bank")
+                if h == 0:
+                    out_bank[h, i] = psum_s.tile([P, D], F32, name="s_bank", tag="s_bank")
+                else:
+                    out_bank[h, i] = psum_q.tile([P, D], F32, name="q_bank", tag="q_bank")
             multiply(out_bank[h, i][:], f"pg{h}{gg}", i * P, f"dvg{gg}", gg == 0, gg == 1)
 
         def store(h, i, copy):
@@ -416,27 +419,27 @@ def tile_learnedstencilwenostep_kernel(tc, x, cs, ss_bytes, ss_scale, gamma, g, 
                 last = u + 2 == len(UNITS)
                 candidates(u)
                 candidates(u + 1)
+                if u == 12:
+                    pack_pg(1, 0, 0, PASS // 2, nc.gpsimd.tensor_tensor)
                 weigh(u)
                 weigh(u + 1)
-                blend_and_lift(u, "scalar" if last else "gpsimd")
-                blend_and_lift(u + 1, "scalar" if last else "gpsimd")
+                blend_and_lift(u, "scalar" if u >= 12 else "gpsimd")
+                blend_and_lift(u + 1, "scalar" if u >= 12 else "gpsimd")
                 if not last:
                     for i in (u - FIRST_BATCH, u - FIRST_BATCH + 1):
                         divergence(0, i, 0)
                         divergence(0, i, 1)
                         store(0, i, nc.scalar.copy)
-            pack_pg(1, 0)
+            pack_pg(1, 0, PASS // 2, PASS)
 
-            pack_pg(1, 1, 0, P)
             quantise("pg10")
-            for i in range(3):
+            pack_pg(1, 1, 0, P)
+            for i in range(PACK):
                 divergence(1, i, 0)
             for i in range(1, PACK):
                 pack_pg(1, 1, i * P, (i + 1) * P)
                 quantise("pg11", (i - 1) * P, i * P)
             quantise("pg11", 3 * P, PASS)
             for i in range(PACK):
-                if i == 3:
-                    divergence(1, i, 0)
                 divergence(1, i, 1)
                 store(1, i, (nc.scalar.copy, nc.vector.tensor_copy)[i % 2])

from contextlib import ExitStack

import concourse.mybir as mybir
from concourse.masks import make_identity

B, D, F = 1024, 512, 1024
FLOPS = 5 * 2 * B * D * F

F32 = mybir.dt.float32
BF16 = mybir.dt.bfloat16
U32 = mybir.dt.uint32
U8 = mybir.dt.uint8
FP8 = mybir.dt.float8_e4m3fn
FP8X4 = mybir.dt.float8_e4m3fn_x4
ALU = mybir.AluOpType
ACT = mybir.ActivationFunctionType

P = 128
PACK = 4
PASS = P * PACK
RUN = 8

UNITS = [(h, g, t) for h in range(2) for g in range(2) for t in range(PACK)]
FIRST_BATCH = 10


def tile_learnedstencilwenostep_kernel(tc, x, cs, ss_bytes, ss_scale, gamma, g, dv, out):
    nc = tc.nc
    gain = g

    with ExitStack() as ctx:
        keep = ctx.enter_context(tc.tile_pool(name="keep", bufs=1))
        stage = ctx.enter_context(tc.tile_pool(name="stage", bufs=3))
        psum_s = ctx.enter_context(tc.psum_pool(name="psum_s", bufs=3))
        psum_q = ctx.enter_context(tc.psum_pool(name="psum_q", bufs=5))

        ident = keep.tile([P, P], F32, name="ident")
        warm = keep.tile([P, 1], F32, name="warm")
        rows = keep.tile([P, PASS], BF16, name="rows")
        rows_by_tile = keep.tile([P, PACK, P], F32, name="rows_by_tile")
        columns = keep.tile([P, 6, PACK], F32, name="columns")
        log_gamma = keep.tile([P, 4, PACK], F32, name="log_gamma")
        log_ratio = keep.tile([P, 2, PACK], F32, name="log_ratio")
        half_gain = keep.tile([P, 2, PACK], F32, name="half_gain")
        byte_scale = keep.tile([P, PACK], F32, name="byte_scale")

        x_raw = [keep.tile([P, PACK, D], BF16, name=f"x_raw{h}") for h in range(2)]
        ss_raw = [keep.tile([P, PACK, F], U8, name=f"ss_raw{k}") for k in range(2)]
        cs_raw = [keep.tile([P, PACK, F], BF16, name=f"cs_raw{k}") for k in range(2)]
        dv_raw = keep.tile([P, 2, PACK, D], BF16, name="dv_raw")

        operands = ["x0", "x1", "s0g0", "s0g1", "s1g0", "s1g1", "c1g0", "c1g1", "n0t0", "n0t1", "dvg0", "dvg1"]
        operands += [f"pg{h}{gg}" for h in range(2) for gg in range(2)]
        codes = {n: keep.tile([P, PASS], U32, name="codes_" + n, align_bytes=64) for n in operands}
        scales = {n: keep.tile([P, PASS], U8, name="scales_" + n, align_bytes=64) for n in operands}
        weight = [keep.tile([P, PASS], F32, name=f"weight{u}") for u in range(len(UNITS))]

        make_identity(nc, ident[:])
        nc.gpsimd.memset(rows[:], 0.0)
        nc.vector.memset(warm[:], 1.0)

        x_view = x.rearrange("(h r i) k -> h r i k", h=2, i=PACK)
        nc.sync.dma_start(out=byte_scale[:], in_=ss_scale.rearrange("o (p j) q -> p (o j q)", j=PACK))
        nc.sync.dma_start(out=ss_raw[0][:], in_=ss_bytes[0].rearrange("(p j) f -> p j f", j=PACK))
        for i in (0, 2):
            nc.sync.dma_start(out=x_raw[0][:, i : i + 2, :], in_=x_view[0, :, i : i + 2, :])
        nc.sync.dma_start(out=ss_raw[1][:], in_=ss_bytes[1].rearrange("(p j) f -> p j f", j=PACK))
        nc.sync.dma_start(out=rows[0:4, :], in_=gamma.rearrange("k (g f) -> (k g) f", g=2))
        nc.sync.dma_start(out=rows[4:6, :], in_=gain.rearrange("(g f) -> g f", g=2))
        for k in range(2):
            nc.sync.dma_start(out=cs_raw[k][:], in_=cs[k].rearrange("(p j) f -> p j f", j=PACK))
        nc.sync.dma_start(out=x_raw[1][:], in_=x_view[1])
        dv_view = dv.rearrange("(g a t b) n -> g t a b n", g=2, t=PACK, b=RUN)
        for gg in range(2):
            for t in range(PACK):
                nc.sync.dma_start(out=dv_raw[:, gg, t, :], in_=dv_view[gg, t])

        packed = {}

        def packed_tile(n):
            if n not in packed:
                packed[n] = stage.tile([P, PACK * PASS], BF16, name="packed", tag="packed", bufs=6, align_bytes=64)
            return packed[n]

        def quantise(n, lo=0, hi=PASS):
            nc.vector.quantize_mx(
                out=codes[n][:, lo:hi].bitcast(FP8X4),
                scales=scales[n][:, lo:hi],
                in_=packed[n][:, PACK * lo : PACK * hi],
            )

        def multiply(acc, stationary, column, moving, start, stop):
            cols = slice(column, column + P)
            nc.tensor.matmul_mx(
                out=acc,
                lhsT=codes[stationary][:, cols].bitcast(FP8X4),
                lhsT_scale=scales[stationary][:, cols],
                rhs=codes[moving][:].bitcast(FP8X4),
                rhs_scale=scales[moving][:],
                start=start,
                stop=stop,
            )

        turned = {}

        def turn_tokens(h, pair):
            bank = psum_s.tile([P, 2, 2, P], F32, name="s_bank", tag="s_bank")
            for i in range(2):
                words = x_raw[h][:, 2 * pair + i, :].bitcast(F32)
                for w in range(2):
                    nc.tensor.transpose(bank[:, i, w, :], words[:, w::2], ident[:])
            turned[h, pair] = bank

        def pack_tokens(h, pair, copy):
            dst = packed_tile(f"x{h}")[:].bitcast(F32)[:, pair * PASS : (pair + 1) * PASS]
            copy(
                out=dst.rearrange("p (i r w) -> p i r w", i=2, w=2),
                in_=turned[h, pair][:].rearrange("p i w r -> p i r w"),
            )

        widened = {}

        def widen(k, gg, js, engine):
            if (k, gg) not in widened:
                widened[k, gg] = stage.tile([P, PACK, PASS], BF16, name="wide", tag="wide", bufs=3)
            for j in js:
                dst = widened[k, gg][:, j, :]
                src = ss_raw[k][:, j, gg * PASS : (gg + 1) * PASS].bitcast(FP8)
                scale = byte_scale[:, j : j + 1]
                if engine == "scalar":
                    nc.scalar.activation(out=dst, in_=src, func=ACT.Copy, scale=scale)
                else:
                    nc.vector.tensor_scalar(out=dst, in0=src, scalar1=scale, scalar2=None, op0=ALU.mult)

        def by_tile(ap):
            return ap.rearrange("p j (a t b) -> p t a j b", t=PACK, b=RUN)

        def packed_by_tile(ap):
            return ap.rearrange("p (t a b j) -> p t a j b", a=P // RUN, b=RUN, j=PACK)

        def pack_ss(k, gg, tiles=slice(0, PACK)):
            n = f"s{k}g{gg}"
            nc.vector.tensor_copy(out=packed_by_tile(packed_tile(n)[:])[:, tiles], in_=by_tile(widened[k, gg][:])[:, tiles])

        def pack_c1(gg):
            nc.vector.tensor_copy(
                out=packed_by_tile(packed_tile(f"c1g{gg}")[:]),
                in_=by_tile(cs_raw[1][:, :, gg * PASS : (gg + 1) * PASS]),
            )

        def pack_n0(pair):
            src = by_tile(cs_raw[0][:])
            dst = packed_tile(f"n0t{pair}")[:].rearrange("p (t a b j) -> p t a j b", t=2, b=RUN, j=PACK)
            for t in range(2):
                nc.vector.tensor_scalar(out=dst[:, t], in0=src[:, 2 * pair + t], scalar1=-1.0, scalar2=None, op0=ALU.mult)

        def pack_dv(gg):
            nc.vector.tensor_copy(
                out=packed_tile(f"dvg{gg}")[:].rearrange("p (c i t) -> p c t i", i=RUN, t=PACK),
                in_=dv_raw[:, gg].rearrange("p t (c i) -> p c t i", i=RUN),
            )

        def sort_rows():
            nc.gpsimd.tensor_scalar(
                out=rows_by_tile[:].rearrange("p t (a b) -> p t a b", b=RUN),
                in0=rows[:].rearrange("p (a t b) -> p t a b", t=PACK, b=RUN),
                scalar1=1.0,
                scalar2=0.0,
                op0=ALU.mult,
                op1=ALU.add,
            )

        def turn_rows():
            bank = psum_s.tile([P, PACK, P], F32, name="s_bank", tag="s_bank")
            for t in range(PACK):
                nc.tensor.transpose(bank[:, t, :], rows_by_tile[:, t, :], ident[:])
            nc.scalar.copy(out=columns[:], in_=bank[:, :, 0:6].rearrange("p t r -> p r t"))

        def clamp_gamma():
            nc.vector.tensor_scalar(out=log_gamma[:], in0=columns[:, 0:4, :], scalar1=2.0**-64, scalar2=None, op0=ALU.max)
            nc.vector.tensor_scalar(out=half_gain[:], in0=columns[:, 4:6, :], scalar1=0.5, scalar2=None, op0=ALU.mult)

        s_bank = {}
        logs = {}

        def indicator(u, k):
            h, gg, t = UNITS[u]
            s_bank[u, k] = psum_s.tile([P, PASS], F32, name="s_bank", tag="s_bank")
            multiply(s_bank[u, k][:], f"s{k}g{gg}", t * P, f"x{h}", True, True)

        def square(u, k):
            if u not in logs:
                logs[u] = stage.tile([P, 2, PASS], F32, name="logs", tag="logs", bufs=5)
            nc.scalar.activation(out=logs[u][:, k, :], in_=s_bank[u, k][:], func=ACT.Square)

        def log(u):
            nc.scalar.activation(out=logs[u][:], in_=logs[u][:], func=ACT.Ln, bias=0.5, scale=1.0)

        def log_difference(u):
            nc.vector.tensor_tensor(out=weight[u][:], in0=logs[u][:, 0, :], in1=logs[u][:, 1, :], op=ALU.subtract)

        def sigmoid(u):
            h, gg, t = UNITS[u]
            nc.scalar.activation(
                out=weight[u][:], in_=weight[u][:], func=ACT.Sigmoid, bias=log_ratio[:, gg, t : t + 1], scale=2.0
            )

        def squared(u, k):
            indicator(u, k)
            square(u, k)

        difference, minus_q0, step, blend, lifted = {}, {}, {}, {}, {}

        def candidates(u):
            h, gg, t = UNITS[u]
            n0, n0_column = f"n0t{t // 2}", (t % 2 * 2 + gg) * P
            difference[u] = psum_q.tile([P, PASS], F32, name="q_bank", tag="q_bank")
            multiply(difference[u][:], f"c1g{gg}", t * P, f"x{h}", True, False)
            multiply(difference[u][:], n0, n0_column, f"x{h}", False, True)
            minus_q0[u] = psum_q.tile([P, PASS], F32, name="q_bank", tag="q_bank")
            multiply(minus_q0[u][:], n0, n0_column, f"x{h}", True, True)

        def weigh(u):
            step[u] = stage.tile([P, PASS], F32, name="step", tag="step", bufs=3)
            nc.vector.tensor_tensor(out=step[u][:], in0=difference[u][:], in1=weight[u][:], op=ALU.mult)

        def blend_and_lift(u, engine):
            h, gg, t = UNITS[u]
            if (h, gg) not in blend:
                blend[h, gg] = stage.tile([P, PACK, PASS], F32, name="blend", tag="blend", bufs=2)
                lifted[h, gg] = stage.tile([P, PACK, PASS], F32, name="lifted", tag="lifted", bufs=2)
            nc.vector.tensor_tensor(out=blend[h, gg][:, t, :], in0=step[u][:], in1=minus_q0[u][:], op=ALU.subtract)
            if engine is not None:
                lift(u, engine)

        def lift(u, engine):
            h, gg, t = UNITS[u]
            dst, src = lifted[h, gg][:, t, :], blend[h, gg][:, t, :]
            half, whole = half_gain[:, gg, t : t + 1], columns[:, 4 + gg, t : t + 1]
            if engine == "scalar":
                nc.scalar.activation(out=dst, in_=src, func=ACT.Identity, scale=half, bias=whole)
            else:
                (nc.gpsimd if engine == "gpsimd" else nc.vector).tensor_scalar(out=dst, in0=src, scalar1=half, scalar2=whole, op0=ALU.mult, op1=ALU.add)

        def pack_pg(h, gg, lo=0, hi=PASS, multiply=nc.vector.tensor_tensor):
            multiply(
                out=packed_tile(f"pg{h}{gg}")[:, PACK * lo : PACK * hi].rearrange("p (c i t) -> p c t i", i=4, t=PACK),
                in0=lifted[h, gg][:, :, lo:hi].rearrange("p t (c i) -> p c t i", i=4),
                in1=blend[h, gg][:, :, lo:hi].rearrange("p t (c i) -> p c t i", i=4),
                op=ALU.mult,
            )

        out_view = out.rearrange("(h r i) d -> h i r d", h=2, i=PACK)
        out_bank = {}

        def divergence(h, i, gg):
            if gg == 0:
                if h == 0:
                    out_bank[h, i] = psum_s.tile([P, D], F32, name="s_bank", tag="s_bank")
                else:
                    out_bank[h, i] = psum_q.tile([P, D], F32, name="q_bank", tag="q_bank")
            multiply(out_bank[h, i][:], f"pg{h}{gg}", i * P, f"dvg{gg}", gg == 0, gg == 1)

        def store(h, i, copy):
            result = stage.tile([P, D], F32, name="result", tag="result", bufs=4)
            copy(out=result[:], in_=out_bank[h, i][:])
            nc.sync.dma_start(out=out_view[h, i], in_=result[:])

        with tc.manual_schedule():
            nc.scalar.activation(out=warm[:], in_=warm[:], func=ACT.Ln)

            widen(0, 0, (0, 1), "vector")
            widen(0, 0, (2, 3), "scalar")
            widen(0, 1, (0, 1), "vector")
            for pair in range(2):
                turn_tokens(0, pair)
                pack_tokens(0, pair, nc.scalar.copy)
            widen(1, 0, (0, 1, 2), "scalar")
            pack_ss(0, 0, slice(0, 2))
            pack_ss(0, 0, slice(2, 4))
            quantise("s0g0", 0, 2 * P)
            quantise("x0")
            quantise("s0g0", 2 * P, PASS)
            widen(1, 0, (3,), "vector")
            widen(0, 1, (2,), "vector")
            for u in range(4):
                squared(u, 0)
            pack_ss(1, 0)
            widen(0, 1, (3,), "vector")
            quantise("s1g0")
            for u in range(2):
                squared(u, 1)
            log(0)
            log(1)
            for u in range(2, 4):
                squared(u, 1)
            log(2)
            log(3)

            widen(1, 1, range(PACK), "vector")
            pack_ss(0, 1)
            pack_ss(1, 1)
            quantise("s0g1")
            quantise("s1g1")
            turn_tokens(1, 0)
            turn_tokens(1, 1)
            pack_tokens(1, 0, nc.vector.tensor_copy)
            pack_tokens(1, 1, nc.vector.tensor_copy)
            log_difference(0)
            quantise("x1")
            sort_rows()
            squared(4, 0)
            squared(4, 1)
            turn_rows()
            log(4)
            log_difference(1)
            log_difference(2)
            log_difference(3)
            clamp_gamma()
            nc.scalar.activation(out=log_gamma[:], in_=log_gamma[:], func=ACT.Ln)

            pack_n0(0)
            log_difference(4)
            pack_n0(1)
            nc.vector.tensor_tensor(out=log_ratio[:], in0=log_gamma[:, 2:4, :], in1=log_gamma[:, 0:2, :], op=ALU.subtract)
            pack_c1(0)
            squared(5, 0)
            squared(5, 1)
            for u in range(6, FIRST_BATCH):
                squared(u, 0)
                log(u - 1)
                squared(u, 1)
            log(FIRST_BATCH - 1)
            log_difference(5)
            quantise("n0t0")
            quantise("n0t1")
            log_difference(6)
            pack_c1(1)
            quantise("c1g0")
            log_difference(7)
            quantise("c1g1")
            pack_dv(0)
            log_difference(8)
            pack_dv(1)
            log_difference(9)
            quantise("dvg0")

            for u in range(FIRST_BATCH):
                sigmoid(u)
            candidates(0)
            candidates(1)
            indicator(10, 0)
            indicator(10, 1)
            indicator(11, 0)
            weigh(0)
            quantise("dvg1")
            blend_and_lift(0, "gpsimd")
            candidates(2)
            weigh(1)
            weigh(2)
            blend_and_lift(1, "gpsimd")
            blend_and_lift(2, "gpsimd")
            candidates(3)
            candidates(4)
            weigh(3)
            weigh(4)
            blend_and_lift(3, "gpsimd")
            blend_and_lift(4, "gpsimd")
            candidates(5)
            square(10, 0)
            square(10, 1)
            square(11, 0)
            squared(11, 1)
            log(10)
            indicator(12, 0)
            candidates(6)
            indicator(12, 1)
            weigh(5)
            weigh(6)
            blend_and_lift(5, "gpsimd")
            blend_and_lift(6, "gpsimd")
            square(12, 0)
            log(11)
            square(12, 1)
            squared(13, 0)
            candidates(7)
            candidates(8)
            pack_pg(0, 0)
            weigh(7)
            log_difference(10)
            quantise("pg00")
            weigh(8)
            blend_and_lift(7, None)
            blend_and_lift(8, "gpsimd")
            lift(7, "vector")
            log(12)
            squared(13, 1)
            squared(14, 0)
            log(13)
            candidates(9)
            squared(14, 1)
            squared(15, 0)
            log(14)
            squared(15, 1)
            log(15)
            log_difference(11)
            log_difference(12)
            weigh(9)
            log_difference(13)
            blend_and_lift(9, "gpsimd")
            pack_pg(0, 1)
            log_difference(14)
            quantise("pg01")
            log_difference(15)

            for u in range(FIRST_BATCH, len(UNITS)):
                sigmoid(u)
            for u in range(FIRST_BATCH, len(UNITS), 2):
                last = u + 2 == len(UNITS)
                candidates(u)
                candidates(u + 1)
                if u == 12:
                    pack_pg(1, 0, 0, PASS // 2, nc.gpsimd.tensor_tensor)
                weigh(u)
                weigh(u + 1)
                blend_and_lift(u, "scalar" if u >= 12 else "gpsimd")
                blend_and_lift(u + 1, "scalar" if u >= 12 else "gpsimd")
                if not last:
                    for i in (u - FIRST_BATCH, u - FIRST_BATCH + 1):
                        divergence(0, i, 0)
                        divergence(0, i, 1)
                        store(0, i, nc.scalar.copy)
            pack_pg(1, 0, PASS // 2, PASS)

            quantise("pg10")
            pack_pg(1, 1, 0, P)
            for i in range(PACK):
                divergence(1, i, 0)
            for i in range(1, PACK):
                pack_pg(1, 1, i * P, (i + 1) * P)
                quantise("pg11", (i - 1) * P, i * P)
            quantise("pg11", 3 * P, PASS)
            for i in range(PACK):
                divergence(1, i, 1)
                store(1, i, (nc.scalar.copy, nc.vector.tensor_copy)[i % 2])
